import numpy as np
import ml_dtypes


def mxq(x, axis, fmt="e4m3"):
    dtype, down = {"e4m3": (ml_dtypes.float8_e4m3fn, 7), "e5m2": (ml_dtypes.float8_e5m2, 14)}[fmt]
    v = np.moveaxis(np.asarray(x, np.float32).astype(ml_dtypes.bfloat16).astype(np.float64), axis, -1)
    blocks = v.reshape(v.shape[:-1] + (-1, 32))
    amax = np.abs(blocks).max(-1, keepdims=True)
    byte = np.maximum(np.where(amax > 0, np.frexp(amax)[1] - 1 + 127, 0) - down, 1)
    scale = np.exp2(byte - 127.0)
    codes = (blocks / scale).astype(np.float32).astype(dtype).astype(np.float64)
    return np.moveaxis((codes * scale).reshape(v.shape), -1, axis)


WIDE = False


def mx_kscale(k):
    if not WIDE:
        return np.ones(k)
    levels = np.array([10, -10, 5, -5, 0])
    if k % 512:
        return np.exp2(np.random.permutation(np.resize(levels, k // 32))).repeat(32)
    a = np.empty((k // 512, 16))
    for p in range(k // 512):
        a[p, :8] = np.random.permutation(np.resize(levels, 8))
        for g in range(8):
            far = levels[np.abs(levels - a[p, g]) >= 10]
            a[p, g + 8] = far[np.random.randint(len(far))]
    return np.exp2(a.ravel()).repeat(32)


BF16 = ml_dtypes.bfloat16


def bf(x):
    return np.asarray(x, np.float32).astype(BF16)


def f64(x):
    return np.asarray(x).astype(np.float64)


E2M1 = np.array([0.0, 0.5, 1.0, 1.5, 2.0, 3.0, 4.0, 6.0, -0.0, -0.5, -1.0, -1.5, -2.0, -3.0, -4.0, -6.0])


def pack_weight(w, fmt):
    k, n = w.shape
    w = f64(bf(w)).reshape(k // 32, 32, n)
    amax = np.abs(w).max(1)
    if fmt == "e4m3":
        byte = np.frexp(amax)[1] - 1 + 127 - 7
    else:
        mant, ex = np.frexp(amax / 6.0)
        byte = np.where(mant > 0.5, ex, ex - 1) + 127
    byte = np.clip(np.where(amax > 0, byte, 1), 1, 254)
    scaled = (w * np.exp2(127.0 - byte)[:, None, :]).reshape(k, n).astype(np.float32)
    by_word = np.ascontiguousarray(scaled.reshape(k // 512, 128, 4, n).transpose(0, 1, 3, 2))
    if fmt == "e4m3":
        words = by_word.astype(ml_dtypes.float8_e4m3fn).view(np.uint8)
    else:
        c = by_word.astype(ml_dtypes.float4_e2m1fn).view(np.uint8) & 0xF
        words = c[..., 0::2] | (c[..., 1::2] << 4)
    return np.ascontiguousarray(words), np.ascontiguousarray(byte.astype(np.uint8).reshape(k // 512, 16, n))


def unpack_weight(words, scales, fmt):
    g, p, n, _ = words.shape
    if fmt == "e4m3":
        vals = np.ascontiguousarray(words).view(ml_dtypes.float8_e4m3fn).astype(np.float64)
    else:
        nib = np.empty((g, p, n, 4), np.uint8)
        nib[..., 0::2] = words & 0xF
        nib[..., 1::2] = words >> 4
        vals = E2M1[nib]
    vals = vals * np.repeat(np.exp2(scales.astype(np.float64) - 127.0), 8, axis=1)[..., None]
    return vals.transpose(0, 1, 3, 2).reshape(g * 512, n)
def pack4(w):
    words, scales = pack_weight(w, "e2m1")
    return words.reshape(words.shape[0], 128, -1), scales


def unpack4(words, scales):
    return unpack_weight(words.reshape(words.shape[0], 128, -1, 2), scales, "e2m1")


N, D, M = 2048, 1024, 1024


def draw0():
    s = mx_kscale(D)
    u = mx_kscale(N)
    x = bf(np.random.standard_normal((N, D)) * s)
    w_words, w_scales = pack4(np.random.standard_normal((D, M)) / np.sqrt(D) / s[:, None])
    return {
        "x": x,
        "w_words": w_words,
        "w_scales": w_scales,
        "c": bf(0.2 * np.random.standard_normal(M)),
        "k": bf(np.random.standard_normal(M)),
        "a": bf((1.0 + 0.3 * np.random.standard_normal(N)) * u),
        "b": bf((1.0 + 0.3 * np.random.standard_normal(N)) / u),
    }


def core(x, w_words, w_scales, c, k, a, b):
    root_n = np.sqrt(x.shape[0])
    w = unpack4(w_words, w_scales)
    y = (mxq(f64(x), 1, "e4m3") @ w) + f64(c)[None, :]
    f = (y + f64(k)[None, :] * np.tanh(y)) * f64(a)[:, None]
    h = y * f64(b)[:, None]
    m = (mxq(f, 0, "e4m3").T @ mxq(h, 0, "e4m3")) / root_n
    return -m + root_n * np.eye(w.shape[1])


def e4m3fn_bytes(y):
    return np.clip(np.asarray(y, np.float64), -448.0, 448.0).astype(np.float32).astype(ml_dtypes.float8_e4m3fn).view(np.uint8)


def e4m3fn_values(b):
    return np.asarray(b, np.uint8).view(ml_dtypes.float8_e4m3fn).astype(np.float64)


def setup_inputs():
    d = draw0()
    x0 = np.asarray(d['x']).astype(np.float64)
    s = (np.max(np.abs(x0), axis=(0,), keepdims=True) / 448.0).astype(np.float32)
    out = {}
    for k, v in d.items():
        if k == 'x':
            out['x_bytes'] = e4m3fn_bytes(x0 / s.astype(np.float64))
            out['x_scale'] = s
        else:
            out[k] = v
    return out


def reference(x_bytes, x_scale, w_words, w_scales, c, k, a, b):
    return core(e4m3fn_values(x_bytes) * x_scale.astype(np.float64), w_words, w_scales, c, k, a, b)

@@ -1,0 +1,394 @@
+import math
+from contextlib import ExitStack
+
+import concourse.mybir as mybir
+from concourse.masks import make_identity
+
+N, D, M = 2048, 1024, 1024
+FLOPS = 2 * N * D * M + 2 * N * M * M
+
+F32 = mybir.dt.float32
+BF16 = mybir.dt.bfloat16
+I32 = mybir.dt.int32
+U32 = mybir.dt.uint32
+U8 = mybir.dt.uint8
+FP8 = mybir.dt.float8_e4m3fn
+FP8X4 = mybir.dt.float8_e4m3fn_x4
+FP4X4 = mybir.dt.float4_e2m1fn_x4
+ALU = mybir.AluOpType
+ACT = mybir.ActivationFunctionType
+
+P = 128
+PASS = 512
+GROUPS = N // PASS
+D_PASSES = D // PASS
+CHUNKS = M // P
+EARLY_CHUNKS = 4
+PE_SUM_UNITS = 10
+
+
+def tile_extendedinfomaxicarelativegrad_w4_kernel(
+    tc, x_bytes, x_scale, w_words, w_scales, c, k, a, b, out
+):
+    nc = tc.nc
+    root_n = math.sqrt(N)
+
+    with ExitStack() as ctx:
+        keep = ctx.enter_context(tc.tile_pool(name="keep", bufs=1))
+        work = ctx.enter_context(tc.tile_pool(name="work", bufs=3))
+        psum = ctx.enter_context(tc.psum_pool(name="psum", bufs=3))
+        ctx.enter_context(tc.manual_schedule())
+
+        ident = keep.tile([P, P], F32)
+        ident_bf = keep.tile([P, P], BF16)
+        root_ident = keep.tile([P, P], F32)
+        ck_rows = keep.tile([P, P], BF16)
+        ck = keep.tile([P, 2 * CHUNKS], F32)
+        scale_cols = keep.tile([P, 8], F32)
+        scale_spread = keep.tile([P, D], F32)
+        a_cols = keep.tile([P, GROUPS * 4], BF16)
+        b_cols = keep.tile([P, GROUPS * 4], BF16)
+        a_spread = keep.tile([P, N], BF16)
+        b_spread = keep.tile([P, N], BF16)
+        w_codes = keep.tile([P, D_PASSES, 2 * M], U8, align_bytes=64)
+        w_plane = keep.tile([P, D_PASSES, M], U8, align_bytes=64)
+        x_codes = keep.tile([P, D_PASSES, N], U32, align_bytes=64)
+        x_plane = keep.tile([P, D_PASSES, N], U8, align_bytes=64)
+        f_codes = keep.tile([P, GROUPS, M], U32, align_bytes=64)
+        f_plane = keep.tile([P, GROUPS, M], U8, align_bytes=64)
+        h_codes = keep.tile([P, GROUPS, M], U32, align_bytes=64)
+        h_plane = keep.tile([P, GROUPS, M], U8, align_bytes=64)
+
+        x_raw = {}
+
+        def load_x(g, u):
+            x_raw[g, u] = keep.tile([P, 2, D], U8, name="x_raw_%d_%d" % (g, u))
+            rows = x_bytes[g * PASS : (g + 1) * PASS, :].rearrange("(p t) d -> p t d", t=4)
+            nc.sync.dma_start(out=x_raw[g, u][:], in_=rows[:, 2 * u : 2 * u + 2, :])
+
+        nc.vector.memset(ck_rows[:], 0.0)
+        nc.vector.memset(w_plane[:].rearrange("p g n -> p (g n)").bitcast(I32), 0)
+        make_identity(nc, ident[:])
+        make_identity(nc, ident_bf[:])
+
+        nc.sync.dma_start(out=scale_cols[:], in_=x_scale.rearrange("o (p j) -> p (o j)", j=8))
+        for g in range(2):
+            load_x(g, 0)
+            load_x(g, 1)
+        nc.sync.dma_start(
+            out=a_cols[:].rearrange("p (g t) -> p g t", t=4), in_=a.rearrange("(g p t) -> p g t", p=P, t=4)
+        )
+        nc.sync.dma_start(
+            out=b_cols[:].rearrange("p (g t) -> p g t", t=4), in_=b.rearrange("(g p t) -> p g t", p=P, t=4)
+        )
+        nc.sync.dma_start(out=ck_rows[0:CHUNKS, :], in_=c.rearrange("(j p) -> j p", p=P))
+        nc.sync.dma_start(out=ck_rows[CHUNKS : 2 * CHUNKS, :], in_=k.rearrange("(j p) -> j p", p=P))
+        nc.sync.dma_start(out=w_codes[:].bitcast(I32), in_=w_words.rearrange("g p n -> p g n").bitcast(I32))
+        for q in range(4):
+            nc.sync.dma_start(
+                out=w_plane[32 * q : 32 * q + 4, :, :].bitcast(I32),
+                in_=w_scales[:, 4 * q : 4 * q + 4, :].rearrange("g r n -> r g n").bitcast(I32),
+            )
+        for g in range(2, GROUPS):
+            load_x(g, 0)
+            load_x(g, 1)
+
+        def spread_bank(cols, first):
+            bank = psum.tile([P, 4, P], F32, tag="misc")
+            for i in range(4):
+                nc.tensor.transpose(bank[:, i, :], cols[:, first + i : first + i + 1].to_broadcast([P, P]), ident[:])
+            return bank
+
+        for half in range(2):
+            bank = spread_bank(scale_cols, 4 * half)
+            dst = scale_spread[:].rearrange("q (p j) -> q p j", j=8)[:, :, 4 * half : 4 * half + 4]
+            if half == 0:
+                nc.scalar.copy(out=dst, in_=bank[:].rearrange("q j p -> q p j"))
+            else:
+                nc.vector.tensor_copy(out=dst, in_=bank[:].rearrange("q j p -> q p j"))
+
+        def spread_pairs(cols, spread, half):
+            bank = spread_bank(cols[:].bitcast(F32), 4 * half)
+            nc.scalar.copy(
+                out=spread[:].bitcast(F32)[:, PASS * half : PASS * (half + 1)], in_=bank[:].rearrange("q i p -> q (i p)")
+            )
+
+        def turn_ck():
+            bank = psum.tile([P, P], BF16, tag="misc")
+            nc.tensor.transpose(bank[:], ck_rows[:], ident_bf[:])
+            nc.scalar.copy(out=ck[:], in_=bank[:, 0 : 2 * CHUNKS])
+
+        x_wide, x_grouped, x_bank = {}, {}, {}
+
+        def scale_x(g, t):
+            u, e = divmod(t, 2)
+            if e == 0:
+                x_wide[g, u] = work.tile([P, 2, D], BF16, name="x_wide")
+            nc.vector.tensor_tensor(
+                out=x_wide[g, u][:, e, :], in0=x_raw[g, u][:, e, :].bitcast(FP8), in1=scale_spread[:], op=ALU.mult
+            )
+
+        def turn_x(g, u, s):
+            words = x_wide[g, u][:].bitcast(F32)
+            x_bank[g, u, s] = psum.tile([P, 4, P], F32, name="x_bank", tag="misc")
+            for e in range(2):
+                for v in range(2):
+                    nc.tensor.transpose(
+                        x_bank[g, u, s][:, 2 * e + v, :], words[:, e, 256 * s + v : 256 * (s + 1) : 2], ident[:]
+                    )
+
+        def group_x(g, u, s):
+            if u == 0:
+                x_grouped[g, s] = work.tile([P, 4 * PASS], BF16, name="x_grouped", bufs=4, align_bytes=64)
+            dst = x_grouped[g, s][:].bitcast(F32)[:, PASS * u : PASS * (u + 1)]
+            nc.scalar.copy(
+                out=dst.rearrange("p (q j) -> p q j", j=4), in_=x_bank[g, u, s][:].rearrange("p j q -> p q j")
+            )
+
+        def quantize_x(g, s):
+            cols = slice(g * PASS, (g + 1) * PASS)
+            nc.vector.quantize_mx(
+                out=x_codes[:, s, cols].bitcast(FP8X4), scales=x_plane[:, s, cols], in_=x_grouped[g, s][:]
+            )
+
+        units = [(g, j) for g in range(GROUPS) for j in range(EARLY_CHUNKS)]
+        units = units + [(g, j) for j in range(EARLY_CHUNKS, CHUNKS) for g in range(GROUPS)]
+        y_bank, tanh_y, y_full, k_tanh, u_sum, f_rows, h_rows, turned, h_turned, grouped = (
+            {}, {}, {}, {}, {}, {}, {}, {}, {}, {},
+        )
+
+        def live(n):
+            return 0 <= n < len(units)
+
+        def pe_sum(n):
+            return n < PE_SUM_UNITS
+
+        def project(n):
+            g, j = units[n]
+            y_bank[n] = psum.tile([P, PASS], F32, name="y_bank")
+            for s in range(D_PASSES):
+                nc.tensor.matmul_mx(
+                    out=y_bank[n][:],
+                    lhsT=w_codes[:, s, 2 * P * j : 2 * P * (j + 1)].bitcast(FP4X4),
+                    lhsT_scale=w_plane[:, s, P * j : P * (j + 1)],
+                    rhs=x_codes[:, s, g * PASS : (g + 1) * PASS].bitcast(FP8X4),
+                    rhs_scale=x_plane[:, s, g * PASS : (g + 1) * PASS],
+                    start=(s == 0),
+                    stop=(s == D_PASSES - 1),
+                )
+
+        def activate(n):
+            g, j = units[n]
+            c_col = ck[:, j : j + 1]
+            tanh_y[n] = work.tile([P, PASS], F32, name="tanh_y")
+            if not pe_sum(n):
+                nc.scalar.activation(out=tanh_y[n][:], in_=y_bank[n][:], func=ACT.Tanh, bias=c_col)
+                return
+            by_slot = y_bank[n][:].rearrange("m (u p e) -> m u e p", u=2, e=2)
+            y_full[n] = work.tile([P, PASS], F32, name="y_full")
+            k_tanh[n] = work.tile([P, PASS], F32, name="k_tanh")
+            nc.scalar.activation(
+                out=tanh_y[n][:].rearrange("m (u e p) -> m u e p", u=2, e=2), in_=by_slot, func=ACT.Tanh, bias=c_col
+            )
+            nc.scalar.activation(
+                out=y_full[n][:].rearrange("m (u e p) -> m u e p", u=2, e=2), in_=by_slot, func=ACT.Identity, bias=c_col
+            )
+            nc.scalar.activation(
+                out=k_tanh[n][:], in_=tanh_y[n][:], func=ACT.Copy, scale=ck[:, CHUNKS + j : CHUNKS + j + 1]
+            )
+
+        def make_h(n):
+            g, j = units[n]
+            h_rows[n] = work.tile([P, PASS], BF16, name="h_rows", bufs=4)
+            nc.vector.scalar_tensor_tensor(
+                out=h_rows[n][:], in0=y_bank[n][:], scalar=ck[:, j : j + 1],
+                in1=b_spread[:, g * PASS : (g + 1) * PASS], op0=ALU.add, op1=ALU.mult,
+            )
+
+        def make_u(n):
+            g, j = units[n]
+            u_sum[n] = work.tile([P, PASS], F32, name="u_sum")
+            nc.vector.scalar_tensor_tensor(
+                out=u_sum[n][:], in0=tanh_y[n][:], scalar=ck[:, CHUNKS + j : CHUNKS + j + 1],
+                in1=y_bank[n][:], op0=ALU.mult, op1=ALU.add,
+            )
+
+        def make_f(n):
+            g, j = units[n]
+            f_rows[n] = work.tile([P, PASS], BF16, name="f_rows")
+            nc.vector.scalar_tensor_tensor(
+                out=f_rows[n][:], in0=u_sum[n][:], scalar=ck[:, j : j + 1],
+                in1=a_spread[:, g * PASS : (g + 1) * PASS], op0=ALU.add, op1=ALU.mult,
+            )
+
+        def turn_pairs(rows, bank, first):
+            words = rows[:].bitcast(F32)
+            for u in range(2):
+                nc.tensor.transpose(bank[:, first + u, :], words[:, P * u : P * (u + 1)], ident[:])
+
+        def turn_fh(n):
+            turned[n] = psum.tile([P, 4, P], F32, name="turned", bufs=2)
+            turn_pairs(f_rows[n], turned[n], 0)
+            turn_pairs(h_rows[n], turned[n], 2)
+
+        def new_grouped(n):
+            if n not in grouped:
+                grouped[n] = work.tile([P, 2 * PASS], BF16, name="grouped", bufs=4, align_bytes=64)
+
+        def group_fh(n):
+            new_grouped(n)
+            nc.scalar.copy(
+                out=grouped[n][:].bitcast(F32).rearrange("p (i m u) -> p i m u", i=2, u=2),
+                in_=turned[n][:].rearrange("p (i u) m -> p i m u", u=2),
+            )
+
+        def turn_h(n):
+            h_turned[n] = psum.tile([P, 2, P], F32, name="h_turned", tag="misc")
+            turn_pairs(h_rows[n], h_turned[n], 0)
+
+        def group_h(n):
+            new_grouped(n)
+            nc.scalar.copy(
+                out=grouped[n][:].bitcast(F32)[:, PASS // 2 :].rearrange("p (m u) -> p m u", u=2),
+                in_=h_turned[n][:].rearrange("p u m -> p m u"),
+            )
+
+        def turn_sum(n):
+            turned[n] = psum.tile([P, 4, P], F32, name="turned", bufs=2)
+            for t in range(4):
+                for term, first in ((y_full[n], True), (k_tanh[n], False)):
+                    nc.tensor.matmul(
+                        out=turned[n][:, t, :], lhsT=term[:, P * t : P * (t + 1)], rhs=ident[:],
+                        is_transpose=True, start=first, stop=not first,
+                    )
+
+        def group_f(n):
+            g, j = units[n]
+            new_grouped(n)
+            nc.vector.tensor_tensor(
+                out=grouped[n][:, 0:PASS].rearrange("p (m t) -> p m t", t=4),
+                in0=turned[n][:].rearrange("p t m -> p m t"),
+                in1=a_cols[:, 4 * g : 4 * g + 4].unsqueeze(1).to_broadcast([P, P, 4]),
+                op=ALU.mult,
+            )
+
+        def quantize_fh(n):
+            g, j = units[n]
+            cols = slice(P * j, P * (j + 1))
+            nc.vector.quantize_mx(
+                out=h_codes[:, g, cols].bitcast(FP8X4), scales=h_plane[:, g, cols], in_=grouped[n][:, PASS:]
+            )
+            nc.vector.quantize_mx(
+                out=f_codes[:, g, cols].bitcast(FP8X4), scales=f_plane[:, g, cols], in_=grouped[n][:, 0:PASS]
+            )
+
+        def mx_group(dst, i, col0, width):
+            rows, cols = slice(P * i, P * (i + 1)), slice(col0, col0 + width)
+            for g in range(GROUPS):
+                nc.tensor.matmul_mx(
+                    out=dst,
+                    lhsT=f_codes[:, g, rows].bitcast(FP8X4),
+                    lhsT_scale=f_plane[:, g, rows],
+                    rhs=h_codes[:, g, cols].bitcast(FP8X4),
+                    rhs_scale=h_plane[:, g, cols],
+                    start=(g == 0),
+                    stop=(g == GROUPS - 1),
+                )
+
+        def pieces_of(j):
+            cols = [("col", j, i0, min(4, j - i0)) for i0 in range(0, j, 4)]
+            rows = [("row", j, i0, min(4, j + 1 - i0)) for i0 in range(0, j + 1, 4)]
+            return cols + rows
+
+        def multiply(piece):
+            kind, j, i0, count = piece
+            bank = psum.tile([P, PASS], F32, name="out_bank", tag="misc")
+            if kind == "col":
+                for i in range(count):
+                    mx_group(bank[:, P * i : P * (i + 1)], i0 + i, P * j, P)
+            else:
+                done = 0
+                for width in (4, 2, 1):
+                    if count - done >= width:
+                        mx_group(bank[:, P * done : P * (done + width)], j, P * (i0 + done), P * width)
+                        done = done + width
+            return bank
+
+        def finish(piece, bank):
+            kind, j, i0, count = piece
+            result = work.tile([P, PASS], F32, name="result", bufs=4)
+            plain = count - 1 if kind == "row" and i0 + count == j + 1 else count
+            if plain > 0:
+                nc.scalar.activation(
+                    out=result[:, 0 : P * plain], in_=bank[:, 0 : P * plain], func=ACT.Copy, scale=-1.0 / root_n
+                )
+            if plain < count:
+                nc.vector.scalar_tensor_tensor(
+                    out=result[:, P * plain : P * count], in0=bank[:, P * plain : P * count], scalar=-1.0 / root_n,
+                    in1=root_ident[:], op0=ALU.mult, op1=ALU.add,
+                )
+            if kind == "col":
+                dst = out[P * i0 : P * (i0 + count), P * j : P * (j + 1)].rearrange("(i p) n -> p i n", p=P)
+                nc.sync.dma_start(out=dst, in_=result[:, 0 : P * count].rearrange("p (i n) -> p i n", n=P))
+            else:
+                nc.sync.dma_start(
+                    out=out[P * j : P * (j + 1), P * i0 : P * (i0 + count)], in_=result[:, 0 : P * count]
+                )
+
+        nc.gpsimd.tensor_scalar(
+            out=root_ident[:], in0=ident[:], scalar1=root_n, scalar2=0.0, op0=ALU.mult, op1=ALU.add
+        )
+
+        setup = {-6: lambda: spread_pairs(b_cols, b_spread, 0), -5: turn_ck,
+                 -4: lambda: spread_pairs(a_cols, a_spread, 0), -3: lambda: spread_pairs(b_cols, b_spread, 1),
+                 -2: lambda: spread_pairs(a_cols, a_spread, 1)}
+        waiting, multiplied = [], []
+        for step in range(-9, len(units) + 8):
+            x_stage = [(g, step - EARLY_CHUNKS * g) for g in range(GROUPS)]
+            x_turns = [(g,) + divmod(rel + 7, 2) for g, rel in x_stage if -7 <= rel <= -4]
+            if live(step - 1) and pe_sum(step - 1):
+                turn_h(step - 1)
+            if live(step - 2) and not pe_sum(step - 2):
+                turn_fh(step - 2)
+            for g, u, s in x_turns:
+                turn_x(g, u, s)
+            if live(step) and pe_sum(step):
+                turn_sum(step)
+            if live(step + 2):
+                project(step + 2)
+            ready, multiplied = multiplied, []
+            if live(step + 1):
+                activate(step + 1)
+            if live(step - 1) and pe_sum(step - 1):
+                group_h(step - 1)
+            if live(step - 2) and not pe_sum(step - 2):
+                group_fh(step - 2)
+            for g, u, s in x_turns:
+                group_x(g, u, s)
+            if step in setup:
+                setup[step]()
+            if live(step):
+                make_h(step)
+                if not pe_sum(step):
+                    make_u(step)
+            if live(step - 1):
+                if pe_sum(step - 1):
+                    group_f(step - 1)
+                else:
+                    make_f(step - 1)
+            for g, rel in x_stage:
+                if -9 <= rel <= -6:
+                    scale_x(g, rel + 9)
+            for piece, bank in ready:
+                finish(piece, bank)
+            if waiting:
+                multiplied.append((waiting[0], multiply(waiting[0])))
+                waiting = waiting[1:]
+            if live(step - 3):
+                quantize_fh(step - 3)
+                if units[step - 3][0] == GROUPS - 1:
+                    waiting.extend(pieces_of(units[step - 3][1]))
+            for g, rel in x_stage:
+                if -4 <= rel <= -3:
+                    quantize_x(g, rel + 4)
+        assert not waiting and not multiplied

@@ -1,5 +1,7 @@
 import math
+from collections import defaultdict
 from contextlib import ExitStack
+from functools import partial
 
 import concourse.mybir as mybir
 from concourse.masks import make_identity
@@ -25,6 +27,15 @@ D_PASSES = D // PASS
 CHUNKS = M // P
 EARLY_CHUNKS = 4
 PE_SUM_UNITS = 10
+LAST_LAG = 1
+MX_FIRST_UNTIL = -99
+A1_STEP = 10
+A0_STEP = 12
+X_SHIFT = 0
+POOL_DIAG = 1
+PLAIN_SLOTS = ()
+QUICK_FROM = 12
+COL6_ON_VECTOR = 0
 
 
 def tile_extendedinfomaxicarelativegrad_w4_kernel(
@@ -71,19 +82,23 @@ def tile_extendedinfomaxicarelativegrad_w4_kernel(
         make_identity(nc, ident[:])
         make_identity(nc, ident_bf[:])
 
-        nc.sync.dma_start(out=scale_cols[:], in_=x_scale.rearrange("o (p j) -> p (o j)", j=8))
-        for g in range(2):
-            load_x(g, 0)
-            load_x(g, 1)
         nc.sync.dma_start(
-            out=a_cols[:].rearrange("p (g t) -> p g t", t=4), in_=a.rearrange("(g p t) -> p g t", p=P, t=4)
+            out=scale_cols[:].rearrange("p (s t) -> p s t", t=4),
+            in_=x_scale.rearrange("o (s p t) -> p (o s) t", p=P, t=4),
         )
+        load_x(0, 0)
+        load_x(0, 1)
         nc.sync.dma_start(
             out=b_cols[:].rearrange("p (g t) -> p g t", t=4), in_=b.rearrange("(g p t) -> p g t", p=P, t=4)
+        )
+        nc.sync.dma_start(
+            out=a_cols[:].rearrange("p (g t) -> p g t", t=4), in_=a.rearrange("(g p t) -> p g t", p=P, t=4)
         )
         nc.sync.dma_start(out=ck_rows[0:CHUNKS, :], in_=c.rearrange("(j p) -> j p", p=P))
         nc.sync.dma_start(out=ck_rows[CHUNKS : 2 * CHUNKS, :], in_=k.rearrange("(j p) -> j p", p=P))
         nc.sync.dma_start(out=w_codes[:].bitcast(I32), in_=w_words.rearrange("g p n -> p g n").bitcast(I32))
+        load_x(1, 0)
+        load_x(1, 1)
         for q in range(4):
             nc.sync.dma_start(
                 out=w_plane[32 * q : 32 * q + 4, :, :].bitcast(I32),
@@ -93,28 +108,28 @@ def tile_extendedinfomaxicarelativegrad_w4_kernel(
             load_x(g, 0)
             load_x(g, 1)
 
-        def spread_bank(cols, first):
-            bank = psum.tile([P, 4, P], F32, tag="misc")
+        def spread_bank(cols, first, tag):
+            bank = psum.tile([P, 4, P], F32, tag=tag, bufs=1)
             for i in range(4):
                 nc.tensor.transpose(bank[:, i, :], cols[:, first + i : first + i + 1].to_broadcast([P, P]), ident[:])
             return bank
 
         for half in range(2):
-            bank = spread_bank(scale_cols, 4 * half)
-            dst = scale_spread[:].rearrange("q (p j) -> q p j", j=8)[:, :, 4 * half : 4 * half + 4]
-            if half == 0:
-                nc.scalar.copy(out=dst, in_=bank[:].rearrange("q j p -> q p j"))
+            bank = spread_bank(scale_cols, 4 * half, "turn%d" % half)
+            dst = scale_spread[:, PASS * half : PASS * (half + 1)].rearrange("q (p j) -> q p j", j=4)
+            if half == 1:
+                nc.scalar.activation(out=dst, in_=bank[:].rearrange("q j p -> q p j"), func=ACT.Copy)
             else:
                 nc.vector.tensor_copy(out=dst, in_=bank[:].rearrange("q j p -> q p j"))
 
-        def spread_pairs(cols, spread, half):
-            bank = spread_bank(cols[:].bitcast(F32), 4 * half)
+        def spread_pairs(cols, spread, half, tag):
+            bank = spread_bank(cols[:].bitcast(F32), 4 * half, tag)
             nc.scalar.copy(
                 out=spread[:].bitcast(F32)[:, PASS * half : PASS * (half + 1)], in_=bank[:].rearrange("q i p -> q (i p)")
             )
 
         def turn_ck():
-            bank = psum.tile([P, P], BF16, tag="misc")
+            bank = psum.tile([P, P], BF16, tag="turn1", bufs=1)
             nc.tensor.transpose(bank[:], ck_rows[:], ident_bf[:])
             nc.scalar.copy(out=ck[:], in_=bank[:, 0 : 2 * CHUNKS])
 
@@ -130,7 +145,7 @@ def tile_extendedinfomaxicarelativegrad_w4_kernel(
 
         def turn_x(g, u, s):
             words = x_wide[g, u][:].bitcast(F32)
-            x_bank[g, u, s] = psum.tile([P, 4, P], F32, name="x_bank", tag="misc")
+            x_bank[g, u, s] = psum.tile([P, 4, P], F32, name="x_bank", tag="side%d" % (1 + s), bufs=1)
             for e in range(2):
                 for v in range(2):
                     nc.tensor.transpose(
@@ -207,7 +222,7 @@ def tile_extendedinfomaxicarelativegrad_w4_kernel(
 
         def make_u(n):
             g, j = units[n]
-            u_sum[n] = work.tile([P, PASS], F32, name="u_sum")
+            u_sum[n] = work.tile([P, PASS], F32, name="u_sum", bufs=5)
             nc.vector.scalar_tensor_tensor(
                 out=u_sum[n][:], in0=tanh_y[n][:], scalar=ck[:, CHUNKS + j : CHUNKS + j + 1],
                 in1=y_bank[n][:], op0=ALU.mult, op1=ALU.add,
@@ -226,14 +241,14 @@ def tile_extendedinfomaxicarelativegrad_w4_kernel(
             for u in range(2):
                 nc.tensor.transpose(bank[:, first + u, :], words[:, P * u : P * (u + 1)], ident[:])
 
-        def turn_fh(n):
-            turned[n] = psum.tile([P, 4, P], F32, name="turned", bufs=2)
+        def turn_fh(n, tag):
+            turned[n] = psum.tile([P, 4, P], F32, name="turned", tag=tag, bufs=1)
             turn_pairs(f_rows[n], turned[n], 0)
             turn_pairs(h_rows[n], turned[n], 2)
 
         def new_grouped(n):
             if n not in grouped:
-                grouped[n] = work.tile([P, 2 * PASS], BF16, name="grouped", bufs=4, align_bytes=64)
+                grouped[n] = work.tile([P, 2 * PASS], BF16, name="grouped", bufs=6, align_bytes=64)
 
         def group_fh(n):
             new_grouped(n)
@@ -242,24 +257,24 @@ def tile_extendedinfomaxicarelativegrad_w4_kernel(
                 in_=turned[n][:].rearrange("p (i u) m -> p i m u", u=2),
             )
 
-        def turn_h(n):
-            h_turned[n] = psum.tile([P, 2, P], F32, name="h_turned", tag="misc")
-            turn_pairs(h_rows[n], h_turned[n], 0)
+        def turn_some(keys, tag, bufs):
+            bank = psum.tile([P, 4, P], F32, name="turned_some", tag=tag, bufs=bufs)
+            for i, (n, half) in enumerate(keys):
+                turn_pairs((f_rows, h_rows)[half][n], bank, 2 * i)
+                h_turned[n, half] = bank[:, 2 * i : 2 * i + 2, :]
 
-        def group_h(n):
+        def group_one(n, half):
             new_grouped(n)
-            nc.scalar.copy(
-                out=grouped[n][:].bitcast(F32)[:, PASS // 2 :].rearrange("p (m u) -> p m u", u=2),
-                in_=h_turned[n][:].rearrange("p u m -> p m u"),
-            )
+            words = grouped[n][:].bitcast(F32)[:, half * PASS // 2 : (half + 1) * PASS // 2]
+            nc.scalar.copy(out=words.rearrange("p (m u) -> p m u", u=2), in_=h_turned[n, half].rearrange("p u m -> p m u"))
 
         def turn_sum(n):
-            turned[n] = psum.tile([P, 4, P], F32, name="turned", bufs=2)
+            turned[n] = psum.tile([P, 4, P], F32, name="turned", tag="turn%d" % (n % 2), bufs=1)
             for t in range(4):
                 for term, first in ((y_full[n], True), (k_tanh[n], False)):
                     nc.tensor.matmul(
                         out=turned[n][:, t, :], lhsT=term[:, P * t : P * (t + 1)], rhs=ident[:],
-                        is_transpose=True, start=first, stop=not first,
+                        is_transpose=not (first and t in PLAIN_SLOTS), start=first, stop=not first,
                     )
 
         def group_f(n):
@@ -272,123 +287,198 @@ def tile_extendedinfomaxicarelativegrad_w4_kernel(
                 op=ALU.mult,
             )
 
-        def quantize_fh(n):
+        def quantize(n, half):
             g, j = units[n]
             cols = slice(P * j, P * (j + 1))
+            codes, plane = ((f_codes, f_plane), (h_codes, h_plane))[half]
             nc.vector.quantize_mx(
-                out=h_codes[:, g, cols].bitcast(FP8X4), scales=h_plane[:, g, cols], in_=grouped[n][:, PASS:]
-            )
-            nc.vector.quantize_mx(
-                out=f_codes[:, g, cols].bitcast(FP8X4), scales=f_plane[:, g, cols], in_=grouped[n][:, 0:PASS]
+                out=codes[:, g, cols].bitcast(FP8X4), scales=plane[:, g, cols],
+                in_=grouped[n][:, half * PASS : (half + 1) * PASS],
             )
 
-        def mx_group(dst, i, col0, width):
-            rows, cols = slice(P * i, P * (i + 1)), slice(col0, col0 + width)
-            for g in range(GROUPS):
-                nc.tensor.matmul_mx(
-                    out=dst,
-                    lhsT=f_codes[:, g, rows].bitcast(FP8X4),
-                    lhsT_scale=f_plane[:, g, rows],
-                    rhs=h_codes[:, g, cols].bitcast(FP8X4),
-                    rhs_scale=h_plane[:, g, cols],
-                    start=(g == 0),
-                    stop=(g == GROUPS - 1),
-                )
+        out_bank, result = {}, {}
 
-        def pieces_of(j):
-            cols = [("col", j, i0, min(4, j - i0)) for i0 in range(0, j, 4)]
-            rows = [("row", j, i0, min(4, j + 1 - i0)) for i0 in range(0, j + 1, 4)]
-            return cols + rows
+        def mx_pass(dst, i, j0, count, g):
+            rows, cols = slice(P * i, P * (i + 1)), slice(P * j0, P * (j0 + count))
+            nc.tensor.matmul_mx(
+                out=dst,
+                lhsT=f_codes[:, g, rows].bitcast(FP8X4),
+                lhsT_scale=f_plane[:, g, rows],
+                rhs=h_codes[:, g, cols].bitcast(FP8X4),
+                rhs_scale=h_plane[:, g, cols],
+                start=(g == 0),
+                stop=(g == GROUPS - 1),
+            )
 
-        def multiply(piece):
-            kind, j, i0, count = piece
-            bank = psum.tile([P, PASS], F32, name="out_bank", tag="misc")
-            if kind == "col":
-                for i in range(count):
-                    mx_group(bank[:, P * i : P * (i + 1)], i0 + i, P * j, P)
+        def multiply(piece, tag, bufs, groups, blocks=None):
+            i0, rows, j0, cols = piece
+            if piece not in out_bank:
+                out_bank[piece] = psum.tile([P, PASS], F32, name="out_bank", tag=tag, bufs=bufs)
+            for i in blocks or range(rows):
+                for g in groups:
+                    mx_pass(out_bank[piece][:, P * i : P * (i + cols)], i0 + i, j0, cols, g)
+
+        def diagonal(piece):
+            i0, rows, j0, cols = piece
+            hits = [i + j for i in range(rows) for j in range(cols) if i0 + i == j0 + j]
+            return hits[0] if hits else None
+
+        def scale_out(piece, first, last, on_vector=False):
+            if last > first:
+                cols = slice(P * first, P * last)
+                if on_vector:
+                    nc.vector.tensor_scalar(
+                        out=result[piece][:, cols], in0=out_bank[piece][:, cols], scalar1=-1.0 / root_n, scalar2=None,
+                        op0=ALU.mult,
+                    )
+                else:
+                    nc.scalar.activation(
+                        out=result[piece][:, cols], in_=out_bank[piece][:, cols], func=ACT.Copy, scale=-1.0 / root_n
+                    )
+
+        def empty(piece, on_vector=False):
+            count = piece[1] * piece[3]
+            result[piece] = work.tile([P, PASS], F32, name="result", bufs=8)
+            d = diagonal(piece)
+            if d is None or (not on_vector and POOL_DIAG):
+                scale_out(piece, 0, count, on_vector)
             else:
-                done = 0
-                for width in (4, 2, 1):
-                    if count - done >= width:
-                        mx_group(bank[:, P * done : P * (done + width)], j, P * (i0 + done), P * width)
-                        done = done + width
-            return bank
+                scale_out(piece, 0, d, on_vector)
+                scale_out(piece, d + 1, count, on_vector)
 
-        def finish(piece, bank):
-            kind, j, i0, count = piece
-            result = work.tile([P, PASS], F32, name="result", bufs=4)
-            plain = count - 1 if kind == "row" and i0 + count == j + 1 else count
-            if plain > 0:
-                nc.scalar.activation(
-                    out=result[:, 0 : P * plain], in_=bank[:, 0 : P * plain], func=ACT.Copy, scale=-1.0 / root_n
-                )
-            if plain < count:
+        def store(piece, on_vector):
+            i0, rows, j0, cols = piece
+            d = diagonal(piece)
+            if d is not None and not on_vector and POOL_DIAG:
+                block = result[piece][:, P * d : P * (d + 1)]
+                nc.gpsimd.tensor_tensor(out=block, in0=block, in1=root_ident[:], op=ALU.add)
+            elif d is not None:
                 nc.vector.scalar_tensor_tensor(
-                    out=result[:, P * plain : P * count], in0=bank[:, P * plain : P * count], scalar=-1.0 / root_n,
-                    in1=root_ident[:], op0=ALU.mult, op1=ALU.add,
+                    out=result[piece][:, P * d : P * (d + 1)], in0=out_bank[piece][:, P * d : P * (d + 1)],
+                    scalar=-1.0 / root_n, in1=root_ident[:], op0=ALU.mult, op1=ALU.add,
                 )
-            if kind == "col":
-                dst = out[P * i0 : P * (i0 + count), P * j : P * (j + 1)].rearrange("(i p) n -> p i n", p=P)
-                nc.sync.dma_start(out=dst, in_=result[:, 0 : P * count].rearrange("p (i n) -> p i n", n=P))
-            else:
-                nc.sync.dma_start(
-                    out=out[P * j : P * (j + 1), P * i0 : P * (i0 + count)], in_=result[:, 0 : P * count]
-                )
+            dst = out[P * i0 : P * (i0 + rows), P * j0 : P * (j0 + cols)].rearrange("(i p) n -> p i n", p=P)
+            nc.sync.dma_start(out=dst, in_=result[piece][:, 0 : P * rows * cols].rearrange("p (i n) -> p i n", i=rows))
 
         nc.gpsimd.tensor_scalar(
             out=root_ident[:], in0=ident[:], scalar1=root_n, scalar2=0.0, op0=ALU.mult, op1=ALU.add
         )
 
-        setup = {-6: lambda: spread_pairs(b_cols, b_spread, 0), -5: turn_ck,
-                 -4: lambda: spread_pairs(a_cols, a_spread, 0), -3: lambda: spread_pairs(b_cols, b_spread, 1),
-                 -2: lambda: spread_pairs(a_cols, a_spread, 1)}
-        waiting, multiplied = [], []
-        for step in range(-9, len(units) + 8):
-            x_stage = [(g, step - EARLY_CHUNKS * g) for g in range(GROUPS)]
-            x_turns = [(g,) + divmod(rel + 7, 2) for g, rel in x_stage if -7 <= rel <= -4]
-            if live(step - 1) and pe_sum(step - 1):
-                turn_h(step - 1)
-            if live(step - 2) and not pe_sum(step - 2):
-                turn_fh(step - 2)
-            for g, u, s in x_turns:
-                turn_x(g, u, s)
-            if live(step) and pe_sum(step):
-                turn_sum(step)
-            if live(step + 2):
-                project(step + 2)
-            ready, multiplied = multiplied, []
-            if live(step + 1):
-                activate(step + 1)
-            if live(step - 1) and pe_sum(step - 1):
-                group_h(step - 1)
-            if live(step - 2) and not pe_sum(step - 2):
-                group_fh(step - 2)
-            for g, u, s in x_turns:
-                group_x(g, u, s)
-            if step in setup:
-                setup[step]()
-            if live(step):
-                make_h(step)
-                if not pe_sum(step):
-                    make_u(step)
-            if live(step - 1):
-                if pe_sum(step - 1):
-                    group_f(step - 1)
-                else:
-                    make_f(step - 1)
-            for g, rel in x_stage:
-                if -9 <= rel <= -6:
-                    scale_x(g, rel + 9)
-            for piece, bank in ready:
-                finish(piece, bank)
-            if waiting:
-                multiplied.append((waiting[0], multiply(waiting[0])))
-                waiting = waiting[1:]
-            if live(step - 3):
-                quantize_fh(step - 3)
-                if units[step - 3][0] == GROUPS - 1:
-                    waiting.extend(pieces_of(units[step - 3][1]))
-            for g, rel in x_stage:
-                if -4 <= rel <= -3:
-                    quantize_x(g, rel + 4)
-        assert not waiting and not multiplied
+        TURN, MX, TANH, EMPTY, GROUP, READ_Y, MAKE_F, SCALE_X, STORE, QUANT, LATE_F = range(11)
+        plan = defaultdict(list)
+
+        def at(step, slot, fn, *args):
+            plan[step, slot].append(partial(fn, *args))
+
+        for g in range(GROUPS):
+            first = EARLY_CHUNKS * g
+            for t in range(4):
+                at(first - 9 + t - (X_SHIFT if g >= 2 and t == 0 else 0), SCALE_X, scale_x, g, t)
+            for u in range(2):
+                for s in range(D_PASSES):
+                    at(first - 7 + 2 * u + s, TURN, turn_x, g, u, s)
+                    at(first - 7 + 2 * u + s, GROUP, group_x, g, u, s)
+            for s in range(D_PASSES):
+                at(first - 4 + s, QUANT, quantize_x, g, s)
+        at(-9, GROUP, spread_pairs, b_cols, b_spread, 0, "side0")
+        at(-9, GROUP, spread_pairs, b_cols, b_spread, 1, "turn0")
+        at(-8, GROUP, turn_ck)
+        at(A1_STEP, GROUP, spread_pairs, a_cols, a_spread, 1, "turn%d" % (PE_SUM_UNITS % 2))
+        at(A0_STEP, GROUP, spread_pairs, a_cols, a_spread, 0, "turn1")
+
+        last_chunk = len(units) - GROUPS
+        for n in range(len(units)):
+            at(n - 2, MX, project, n)
+            at(n - 1, TANH, activate, n)
+            at(n, READ_Y, make_h, n)
+            if pe_sum(n):
+                at(n, TURN, turn_sum, n)
+                at(n + 1, MAKE_F, group_f, n)
+                at(n + 1, TURN, turn_some, [(n, 1)], "side0", 1)
+                at(n + 1, GROUP, group_one, n, 1)
+                at(n + 3, QUANT, quantize, n, 1)
+                at(n + 3, QUANT, quantize, n, 0)
+                continue
+            at(n, READ_Y, make_u, n)
+            hurry = n in (last_chunk - 1, len(units) - 1)
+            f_step = n if hurry else n + 1
+            at(f_step, LATE_F if hurry else MAKE_F, make_f, n)
+            if n < last_chunk:
+                at(f_step + 1, TURN, turn_fh, n, "turn1" if hurry else "turn0")
+                at(f_step + 1, GROUP, group_fh, n)
+                at(f_step + 2 - (n >= QUICK_FROM), QUANT, quantize, n, 1)
+                at(f_step + 2 - (n >= QUICK_FROM), QUANT, quantize, n, 0)
+            else:
+                at(n + 1, TURN, turn_some, [(n, 1)] + [(n - 1, 0)] * (n > last_chunk), "turn0", 1)
+                at(n + 1, GROUP, group_one, n, 1)
+                at(n + 1, QUANT, quantize, n, 1)
+                if hurry:
+                    at(n + 1, TURN, turn_some, [(n, 0)], "y_bank", 3)
+                at(f_step + 1, GROUP, group_one, n, 0)
+                at(f_step + 1, QUANT, quantize, n, 0)
+
+        def finish(step, piece, on_vector=False):
+            at(step, STORE if on_vector else EMPTY, empty, piece, on_vector)
+            at(step, STORE, store, piece, on_vector)
+
+        early = EARLY_CHUNKS * GROUPS
+        for i, tag in enumerate(("side1", "side2", "side0", "turn1")):
+            piece = (i, 1, 0, EARLY_CHUNKS)
+            at(early - 5 + i, MX, multiply, piece, tag, 1, [0, 1])
+            at(early - 1 + i // 2, MX, multiply, piece, tag, 1, [2])
+        for i in (0, 2, 1, 3):
+            piece = (i, 1, 0, EARLY_CHUNKS)
+            at(early + 2, MX, multiply, piece, None, 1, [3])
+            finish(early + 3 + i % 2, piece)
+        for j in range(EARLY_CHUNKS, CHUNKS - 1):
+            first = GROUPS * j
+            row_pieces, done = [], 0
+            for width in (4, 2, 1):
+                if j + 1 - done >= width and len(row_pieces) < 2:
+                    row_pieces.append((j, 1, done, width))
+                    done = done + width
+            hurry = j == CHUNKS - 2
+            for r, piece in enumerate(row_pieces):
+                for step, groups in ((4, [0]), (5, [1, 2, 3])) if hurry else ((4, [0, 1]), (5, [2]), (6, [3])):
+                    at(first + step, MX, multiply, piece, "side%d" % r, 1, groups)
+                finish(first + 7 - hurry, piece)
+            col_rows = j if done == j + 1 else j + 1
+            full, rest = (0, 4, j, 1), (4, col_rows - 4, j, 1)
+            if hurry:
+                at(first + 6, MX, multiply, full, "side2", 1, range(GROUPS))
+                at(first + 6, MX, multiply, rest, "turn1", 1, range(GROUPS), [0])
+                at(first + 7, MX, multiply, rest, "turn1", 1, range(GROUPS), [1, 2])
+                finish(first + 7, full)
+                finish(first + 8, rest)
+            else:
+                if rest[1]:
+                    at(first + 6, MX, multiply, rest, "turn1", 1, range(GROUPS))
+                    finish(first + 7, rest)
+                at(first + 6, MX, multiply, full, "side2", 1, range(GROUPS), range(2 - rest[1]))
+                at(first + 7, MX, multiply, full, "side2", 1, range(GROUPS), range(2 - rest[1], 4))
+                finish(first + 8, full)
+        j = CHUNKS - 1
+        row_pieces = [(j, 1, 0, 4), (j, 1, 4, 4)]
+        col_pieces = [(0, 4, j, 1), (4, 3, j, 1)]
+        end = len(units) + 1
+        for r, piece in enumerate(row_pieces):
+            at(end - 2, MX, multiply, piece, "side%d" % r, 1, [0])
+            at(end - 1, MX, multiply, piece, "side%d" % r, 1, [1])
+        at(end, MX, multiply, col_pieces[0], "y_bank", 3, range(GROUPS))
+        for piece in reversed(row_pieces):
+            at(end, MX, multiply, piece, None, None, [2, 3])
+        at(end, MX, multiply, col_pieces[1], "y_bank", 3, range(GROUPS))
+        finish(end + 1, col_pieces[0])
+        finish(end + 1, row_pieces[1], True)
+        finish(end + 1, row_pieces[0])
+        finish(end + 2, col_pieces[1], True)
+
+        steps = [step for step, slot in plan]
+        for step in range(min(steps), max(steps) + 1):
+            order = [TURN, MX] if step >= MX_FIRST_UNTIL else [MX, TURN]
+            rest = list(range(TANH, LATE_F + 1))
+            if True:
+                rest = [TANH, GROUP, EMPTY] + rest[3:]
+            for slot in order + rest:
+                for fn in plan[step, slot]:
+                    fn()

@@ -27,15 +27,16 @@ D_PASSES = D // PASS
 CHUNKS = M // P
 EARLY_CHUNKS = 4
 PE_SUM_UNITS = 10
-LAST_LAG = 1
-MX_FIRST_UNTIL = -99
-A1_STEP = 10
-A0_STEP = 12
-X_SHIFT = 0
-POOL_DIAG = 1
 PLAIN_SLOTS = ()
-QUICK_FROM = 12
-COL6_ON_VECTOR = 0
+SPLIT0 = 1
+A1_STEP = -7
+A0_STEP = -6
+E3 = 1
+QF_EARLY = 99
+R6 = 1
+R7 = 0
+G3 = 18
+ROW2 = 13
 
 
 def tile_extendedinfomaxicarelativegrad_w4_kernel(
@@ -65,8 +66,8 @@ def tile_extendedinfomaxicarelativegrad_w4_kernel(
         w_plane = keep.tile([P, D_PASSES, M], U8, align_bytes=64)
         x_codes = keep.tile([P, D_PASSES, N], U32, align_bytes=64)
         x_plane = keep.tile([P, D_PASSES, N], U8, align_bytes=64)
-        f_codes = keep.tile([P, GROUPS, M], U32, align_bytes=64)
-        f_plane = keep.tile([P, GROUPS, M], U8, align_bytes=64)
+        f_codes = keep.tile([P, CHUNKS, GROUPS * P], U32, align_bytes=64)
+        f_plane = keep.tile([P, CHUNKS, GROUPS * P], U8, align_bytes=64)
         h_codes = keep.tile([P, GROUPS, M], U32, align_bytes=64)
         h_plane = keep.tile([P, GROUPS, M], U8, align_bytes=64)
 
@@ -139,9 +140,11 @@ def tile_extendedinfomaxicarelativegrad_w4_kernel(
             u, e = divmod(t, 2)
             if e == 0:
                 x_wide[g, u] = work.tile([P, 2, D], BF16, name="x_wide")
-            nc.vector.tensor_tensor(
-                out=x_wide[g, u][:, e, :], in0=x_raw[g, u][:, e, :].bitcast(FP8), in1=scale_spread[:], op=ALU.mult
-            )
+            for cols in (slice(0, PASS), slice(PASS, D)) if (g, t) == (0, 0) and SPLIT0 else (slice(0, D),):
+                nc.vector.tensor_tensor(
+                    out=x_wide[g, u][:, e, cols], in0=x_raw[g, u][:, e, cols].bitcast(FP8),
+                    in1=scale_spread[:, cols], op=ALU.mult,
+                )
 
         def turn_x(g, u, s):
             words = x_wide[g, u][:].bitcast(F32)
@@ -168,15 +171,17 @@ def tile_extendedinfomaxicarelativegrad_w4_kernel(
 
         units = [(g, j) for g in range(GROUPS) for j in range(EARLY_CHUNKS)]
         units = units + [(g, j) for j in range(EARLY_CHUNKS, CHUNKS) for g in range(GROUPS)]
-        y_bank, tanh_y, y_full, k_tanh, u_sum, f_rows, h_rows, turned, h_turned, grouped = (
-            {}, {}, {}, {}, {}, {}, {}, {}, {}, {},
-        )
-
-        def live(n):
-            return 0 <= n < len(units)
+        y_bank, tanh_y, y_full, k_tanh, summed = {}, {}, {}, {}, {}
+        pair_tiles, turned = {}, {}
 
         def pe_sum(n):
             return n < PE_SUM_UNITS
+
+        def pair_tile(name, n, dtype, count=1):
+            key = (name, n // 2)
+            if key not in pair_tiles:
+                pair_tiles[key] = work.tile([P, 2 * PASS], dtype, name=name, align_bytes=64)
+            return pair_tiles[key][:, PASS * (n % 2) : PASS * (n % 2 + count)]
 
         def project(n):
             g, j = units[n]
@@ -214,96 +219,79 @@ def tile_extendedinfomaxicarelativegrad_w4_kernel(
 
         def make_h(n):
             g, j = units[n]
-            h_rows[n] = work.tile([P, PASS], BF16, name="h_rows", bufs=4)
             nc.vector.scalar_tensor_tensor(
-                out=h_rows[n][:], in0=y_bank[n][:], scalar=ck[:, j : j + 1],
+                out=pair_tile("h_rows", n, BF16), in0=y_bank[n][:], scalar=ck[:, j : j + 1],
                 in1=b_spread[:, g * PASS : (g + 1) * PASS], op0=ALU.add, op1=ALU.mult,
             )
 
         def make_u(n):
             g, j = units[n]
-            u_sum[n] = work.tile([P, PASS], F32, name="u_sum", bufs=5)
             nc.vector.scalar_tensor_tensor(
-                out=u_sum[n][:], in0=tanh_y[n][:], scalar=ck[:, CHUNKS + j : CHUNKS + j + 1],
+                out=pair_tile("u_sum", n, F32), in0=tanh_y[n][:], scalar=ck[:, CHUNKS + j : CHUNKS + j + 1],
                 in1=y_bank[n][:], op0=ALU.mult, op1=ALU.add,
             )
 
-        def make_f(n):
+        def make_f(n, count):
             g, j = units[n]
-            f_rows[n] = work.tile([P, PASS], BF16, name="f_rows")
             nc.vector.scalar_tensor_tensor(
-                out=f_rows[n][:], in0=u_sum[n][:], scalar=ck[:, j : j + 1],
-                in1=a_spread[:, g * PASS : (g + 1) * PASS], op0=ALU.add, op1=ALU.mult,
+                out=pair_tile("f_rows", n, BF16, count), in0=pair_tile("u_sum", n, F32, count), scalar=ck[:, j : j + 1],
+                in1=a_spread[:, g * PASS : (g + count) * PASS], op0=ALU.add, op1=ALU.mult,
             )
 
-        def turn_pairs(rows, bank, first):
-            words = rows[:].bitcast(F32)
-            for u in range(2):
-                nc.tensor.transpose(bank[:, first + u, :], words[:, P * u : P * (u + 1)], ident[:])
+        def turn_pair(which, n, tag):
+            words = pair_tile(which + "_rows", n, BF16, 2).bitcast(F32)
+            turned[which, n] = psum.tile([P, 4, P], F32, name="turned", tag=tag, bufs=1)
+            for i in range(4):
+                nc.tensor.transpose(turned[which, n][:, i, :], words[:, P * i : P * (i + 1)], ident[:])
 
-        def turn_fh(n, tag):
-            turned[n] = psum.tile([P, 4, P], F32, name="turned", tag=tag, bufs=1)
-            turn_pairs(f_rows[n], turned[n], 0)
-            turn_pairs(h_rows[n], turned[n], 2)
-
-        def new_grouped(n):
-            if n not in grouped:
-                grouped[n] = work.tile([P, 2 * PASS], BF16, name="grouped", bufs=6, align_bytes=64)
-
-        def group_fh(n):
-            new_grouped(n)
+        def group_pair(which, n):
             nc.scalar.copy(
-                out=grouped[n][:].bitcast(F32).rearrange("p (i m u) -> p i m u", i=2, u=2),
-                in_=turned[n][:].rearrange("p (i u) m -> p i m u", u=2),
+                out=pair_tile(which + "_grouped", n, BF16, 2).bitcast(F32).rearrange("p (i m u) -> p i m u", i=2, u=2),
+                in_=turned[which, n][:].rearrange("p (i u) m -> p i m u", u=2),
             )
-
-        def turn_some(keys, tag, bufs):
-            bank = psum.tile([P, 4, P], F32, name="turned_some", tag=tag, bufs=bufs)
-            for i, (n, half) in enumerate(keys):
-                turn_pairs((f_rows, h_rows)[half][n], bank, 2 * i)
-                h_turned[n, half] = bank[:, 2 * i : 2 * i + 2, :]
-
-        def group_one(n, half):
-            new_grouped(n)
-            words = grouped[n][:].bitcast(F32)[:, half * PASS // 2 : (half + 1) * PASS // 2]
-            nc.scalar.copy(out=words.rearrange("p (m u) -> p m u", u=2), in_=h_turned[n, half].rearrange("p u m -> p m u"))
 
         def turn_sum(n):
-            turned[n] = psum.tile([P, 4, P], F32, name="turned", tag="turn%d" % (n % 2), bufs=1)
+            summed[n] = psum.tile([P, 4, P], F32, name="summed", tag="turn%d" % (n % 2), bufs=1)
             for t in range(4):
                 for term, first in ((y_full[n], True), (k_tanh[n], False)):
                     nc.tensor.matmul(
-                        out=turned[n][:, t, :], lhsT=term[:, P * t : P * (t + 1)], rhs=ident[:],
+                        out=summed[n][:, t, :], lhsT=term[:, P * t : P * (t + 1)], rhs=ident[:],
                         is_transpose=not (first and t in PLAIN_SLOTS), start=first, stop=not first,
                     )
 
         def group_f(n):
             g, j = units[n]
-            new_grouped(n)
             nc.vector.tensor_tensor(
-                out=grouped[n][:, 0:PASS].rearrange("p (m t) -> p m t", t=4),
-                in0=turned[n][:].rearrange("p t m -> p m t"),
+                out=pair_tile("f_grouped", n, BF16).rearrange("p (m t) -> p m t", t=4),
+                in0=summed[n][:].rearrange("p t m -> p m t"),
                 in1=a_cols[:, 4 * g : 4 * g + 4].unsqueeze(1).to_broadcast([P, P, 4]),
                 op=ALU.mult,
             )
 
-        def quantize(n, half):
+        def quantize_f(n, count):
             g, j = units[n]
-            cols = slice(P * j, P * (j + 1))
-            codes, plane = ((f_codes, f_plane), (h_codes, h_plane))[half]
+            cols = slice(P * g, P * (g + count))
             nc.vector.quantize_mx(
-                out=codes[:, g, cols].bitcast(FP8X4), scales=plane[:, g, cols],
-                in_=grouped[n][:, half * PASS : (half + 1) * PASS],
+                out=f_codes[:, j, cols].bitcast(FP8X4), scales=f_plane[:, j, cols],
+                in_=pair_tile("f_grouped", n, BF16, count),
+            )
+
+        def quantize_h(n, count):
+            g, j = units[n]
+            cols = slice(P * j, P * (j + count))
+            nc.vector.quantize_mx(
+                out=h_codes[:, g, cols].bitcast(FP8X4), scales=h_plane[:, g, cols],
+                in_=pair_tile("h_grouped", n, BF16, count),
             )
 
         out_bank, result = {}, {}
 
         def mx_pass(dst, i, j0, count, g):
-            rows, cols = slice(P * i, P * (i + 1)), slice(P * j0, P * (j0 + count))
+            rows, cols = slice(P * g, P * (g + 1)), slice(P * j0, P * (j0 + count))
             nc.tensor.matmul_mx(
                 out=dst,
-                lhsT=f_codes[:, g, rows].bitcast(FP8X4),
-                lhsT_scale=f_plane[:, g, rows],
+                lhsT=f_codes[:, i, rows].bitcast(FP8X4),
+                lhsT_scale=f_plane[:, i, rows],
                 rhs=h_codes[:, g, cols].bitcast(FP8X4),
                 rhs_scale=h_plane[:, g, cols],
                 start=(g == 0),
@@ -340,7 +328,7 @@ def tile_extendedinfomaxicarelativegrad_w4_kernel(
             count = piece[1] * piece[3]
             result[piece] = work.tile([P, PASS], F32, name="result", bufs=8)
             d = diagonal(piece)
-            if d is None or (not on_vector and POOL_DIAG):
+            if d is None or not on_vector:
                 scale_out(piece, 0, count, on_vector)
             else:
                 scale_out(piece, 0, d, on_vector)
@@ -349,7 +337,7 @@ def tile_extendedinfomaxicarelativegrad_w4_kernel(
         def store(piece, on_vector):
             i0, rows, j0, cols = piece
             d = diagonal(piece)
-            if d is not None and not on_vector and POOL_DIAG:
+            if d is not None and not on_vector:
                 block = result[piece][:, P * d : P * (d + 1)]
                 nc.gpsimd.tensor_tensor(out=block, in0=block, in1=root_ident[:], op=ALU.add)
             elif d is not None:
@@ -364,7 +352,7 @@ def tile_extendedinfomaxicarelativegrad_w4_kernel(
             out=root_ident[:], in0=ident[:], scalar1=root_n, scalar2=0.0, op0=ALU.mult, op1=ALU.add
         )
 
-        TURN, MX, TANH, EMPTY, GROUP, READ_Y, MAKE_F, SCALE_X, STORE, QUANT, LATE_F = range(11)
+        TURN, PROJECT, MX, TANH, GROUP, EMPTY, READ_Y, READ_SUM, SCALE_X, QUANT_H, MAKE_F, QUANT, STORE = range(13)
         plan = defaultdict(list)
 
         def at(step, slot, fn, *args):
@@ -373,7 +361,7 @@ def tile_extendedinfomaxicarelativegrad_w4_kernel(
         for g in range(GROUPS):
             first = EARLY_CHUNKS * g
             for t in range(4):
-                at(first - 9 + t - (X_SHIFT if g >= 2 and t == 0 else 0), SCALE_X, scale_x, g, t)
+                at(first - 9 + t, SCALE_X, scale_x, g, t)
             for u in range(2):
                 for s in range(D_PASSES):
                     at(first - 7 + 2 * u + s, TURN, turn_x, g, u, s)
@@ -383,53 +371,52 @@ def tile_extendedinfomaxicarelativegrad_w4_kernel(
         at(-9, GROUP, spread_pairs, b_cols, b_spread, 0, "side0")
         at(-9, GROUP, spread_pairs, b_cols, b_spread, 1, "turn0")
         at(-8, GROUP, turn_ck)
-        at(A1_STEP, GROUP, spread_pairs, a_cols, a_spread, 1, "turn%d" % (PE_SUM_UNITS % 2))
-        at(A0_STEP, GROUP, spread_pairs, a_cols, a_spread, 0, "turn1")
+        at(A1_STEP, GROUP, spread_pairs, a_cols, a_spread, 1, "side0")
+        at(A0_STEP, GROUP, spread_pairs, a_cols, a_spread, 0, "turn0")
 
-        last_chunk = len(units) - GROUPS
+        last = len(units) - 1
         for n in range(len(units)):
-            at(n - 2, MX, project, n)
+            at(n - 2, PROJECT, project, n)
             at(n - 1, TANH, activate, n)
             at(n, READ_Y, make_h, n)
+            if n == last:
+                at(n, READ_Y, make_f, n - 1, 1)
             if pe_sum(n):
                 at(n, TURN, turn_sum, n)
-                at(n + 1, MAKE_F, group_f, n)
-                at(n + 1, TURN, turn_some, [(n, 1)], "side0", 1)
-                at(n + 1, GROUP, group_one, n, 1)
-                at(n + 3, QUANT, quantize, n, 1)
-                at(n + 3, QUANT, quantize, n, 0)
-                continue
-            at(n, READ_Y, make_u, n)
-            hurry = n in (last_chunk - 1, len(units) - 1)
-            f_step = n if hurry else n + 1
-            at(f_step, LATE_F if hurry else MAKE_F, make_f, n)
-            if n < last_chunk:
-                at(f_step + 1, TURN, turn_fh, n, "turn1" if hurry else "turn0")
-                at(f_step + 1, GROUP, group_fh, n)
-                at(f_step + 2 - (n >= QUICK_FROM), QUANT, quantize, n, 1)
-                at(f_step + 2 - (n >= QUICK_FROM), QUANT, quantize, n, 0)
+                at(n + 1, READ_SUM, group_f, n)
             else:
-                at(n + 1, TURN, turn_some, [(n, 1)] + [(n - 1, 0)] * (n > last_chunk), "turn0", 1)
-                at(n + 1, GROUP, group_one, n, 1)
-                at(n + 1, QUANT, quantize, n, 1)
-                if hurry:
-                    at(n + 1, TURN, turn_some, [(n, 0)], "y_bank", 3)
-                at(f_step + 1, GROUP, group_one, n, 0)
-                at(f_step + 1, QUANT, quantize, n, 0)
+                at(n, READ_Y, make_u, n)
+        for n in range(0, len(units), 2):
+            same_chunk = units[n][1] == units[n + 1][1]
+            whole, halves = [(n, 2)], [(n, 1), (n + 1, 1)]
+            at(n + 2, TURN, turn_pair, "h", n, "side0" if pe_sum(n) else "turn1")
+            at(n + 2, GROUP, group_pair, "h", n)
+            if not pe_sum(n):
+                for part in halves[1:] if n + 1 == last else whole if same_chunk else halves:
+                    at(n + 1, MAKE_F, make_f, *part)
+                at(n + 2, TURN, turn_pair, "f", n, "turn0")
+                at(n + 2, GROUP, group_pair, "f", n)
+            for part in halves if same_chunk else whole:
+                at(n + 3, QUANT_H, quantize_h, *part)
+            for part in whole if same_chunk else halves:
+                at(n + 3, QUANT_H if n >= QF_EARLY else QUANT, quantize_f, *part)
 
         def finish(step, piece, on_vector=False):
             at(step, STORE if on_vector else EMPTY, empty, piece, on_vector)
             at(step, STORE, store, piece, on_vector)
 
         early = EARLY_CHUNKS * GROUPS
-        for i, tag in enumerate(("side1", "side2", "side0", "turn1")):
+        for i, tag, step in ((0, "side1", 11), (1, "side2", 11), (2, "side0", ROW2)):
             piece = (i, 1, 0, EARLY_CHUNKS)
-            at(early - 5 + i, MX, multiply, piece, tag, 1, [0, 1])
-            at(early - 1 + i // 2, MX, multiply, piece, tag, 1, [2])
-        for i in (0, 2, 1, 3):
+            at(step, MX, multiply, piece, tag, 1, [0, 1])
+            at(early - 1, MX, multiply, piece, tag, 1, [2])
+        for i in (1, 0, 2):
             piece = (i, 1, 0, EARLY_CHUNKS)
-            at(early + 2, MX, multiply, piece, None, 1, [3])
-            finish(early + 3 + i % 2, piece)
+            at(G3, MX, multiply, piece, None, 1, [3])
+            finish(G3 + 1, piece)
+        piece = (3, 1, 0, EARLY_CHUNKS)
+        at(early + 5, MX, multiply, piece, "side2", 1, range(GROUPS))
+        finish(early + 6, piece)
         for j in range(EARLY_CHUNKS, CHUNKS - 1):
             first = GROUPS * j
             row_pieces, done = [], 0
@@ -438,32 +425,29 @@ def tile_extendedinfomaxicarelativegrad_w4_kernel(
                     row_pieces.append((j, 1, done, width))
                     done = done + width
             hurry = j == CHUNKS - 2
-            for r, piece in enumerate(row_pieces):
-                for step, groups in ((4, [0]), (5, [1, 2, 3])) if hurry else ((4, [0, 1]), (5, [2]), (6, [3])):
-                    at(first + step, MX, multiply, piece, "side%d" % r, 1, groups)
-                finish(first + 7 - hurry, piece)
             col_rows = j if done == j + 1 else j + 1
             full, rest = (0, 4, j, 1), (4, col_rows - 4, j, 1)
-            if hurry:
-                at(first + 6, MX, multiply, full, "side2", 1, range(GROUPS))
-                at(first + 6, MX, multiply, rest, "turn1", 1, range(GROUPS), [0])
-                at(first + 7, MX, multiply, rest, "turn1", 1, range(GROUPS), [1, 2])
-                finish(first + 7, full)
-                finish(first + 8, rest)
-            else:
+            if not hurry:
+                at(first + 7, MX, multiply, full, "side2", 1, range(GROUPS))
+                finish(first + 8 + E3 % 2, full)
                 if rest[1]:
-                    at(first + 6, MX, multiply, rest, "turn1", 1, range(GROUPS))
-                    finish(first + 7, rest)
-                at(first + 6, MX, multiply, full, "side2", 1, range(GROUPS), range(2 - rest[1]))
-                at(first + 7, MX, multiply, full, "side2", 1, range(GROUPS), range(2 - rest[1], 4))
-                finish(first + 8, full)
+                    at(first + 9 + min(E3, 1), MX, multiply, rest, "side2", 1, range(GROUPS))
+                    finish(first + 10 + min(E3, 1), rest)
+            for r, piece in enumerate(row_pieces):
+                at(first + 5, MX, multiply, piece, "side%d" % r, 1, [0, 1])
+                at(first + 7 - hurry, MX, multiply, piece, "side%d" % r, 1, [2, 3])
+                finish(first + 8 - hurry, piece)
+            if hurry:
+                at(first + 6, MX, multiply, full, "y_bank", 3, range(GROUPS))
+                at(first + 7 + R6, MX, multiply, rest, "side2", 1, range(GROUPS))
+                finish(first + 7, full)
+                finish(first + 8 + R6, rest)
         j = CHUNKS - 1
         row_pieces = [(j, 1, 0, 4), (j, 1, 4, 4)]
         col_pieces = [(0, 4, j, 1), (4, 3, j, 1)]
-        end = len(units) + 1
+        end = len(units) + 2
         for r, piece in enumerate(row_pieces):
-            at(end - 2, MX, multiply, piece, "side%d" % r, 1, [0])
-            at(end - 1, MX, multiply, piece, "side%d" % r, 1, [1])
+            at(end - 2 + R7, MX, multiply, piece, "side%d" % r, 1, [0, 1])
         at(end, MX, multiply, col_pieces[0], "y_bank", 3, range(GROUPS))
         for piece in reversed(row_pieces):
             at(end, MX, multiply, piece, None, None, [2, 3])
@@ -473,12 +457,6 @@ def tile_extendedinfomaxicarelativegrad_w4_kernel(
         finish(end + 1, row_pieces[0])
         finish(end + 2, col_pieces[1], True)
 
-        steps = [step for step, slot in plan]
-        for step in range(min(steps), max(steps) + 1):
-            order = [TURN, MX] if step >= MX_FIRST_UNTIL else [MX, TURN]
-            rest = list(range(TANH, LATE_F + 1))
-            if True:
-                rest = [TANH, GROUP, EMPTY] + rest[3:]
-            for slot in order + rest:
-                for fn in plan[step, slot]:
-                    fn()
+        for step, slot in sorted(plan):
+            for fn in plan[step, slot]:
+                fn()

@@ -26,9 +26,10 @@ GROUPS = N // PASS
 D_PASSES = D // PASS
 CHUNKS = M // P
 EARLY_CHUNKS = 4
-PE_SUM_UNITS = 10
-PLAIN_SLOTS = ()
+PE_SUM_UNITS = 12
+PLAIN_SLOTS = (0,)
 SPLIT0 = 1
+KT_DVE = range(8, 12)
 A1_STEP = -7
 A0_STEP = -6
 E3 = 1
@@ -213,8 +214,15 @@ def tile_extendedinfomaxicarelativegrad_w4_kernel(
             nc.scalar.activation(
                 out=y_full[n][:].rearrange("m (u e p) -> m u e p", u=2, e=2), in_=by_slot, func=ACT.Identity, bias=c_col
             )
-            nc.scalar.activation(
-                out=k_tanh[n][:], in_=tanh_y[n][:], func=ACT.Copy, scale=ck[:, CHUNKS + j : CHUNKS + j + 1]
+            if n not in KT_DVE:
+                nc.scalar.activation(
+                    out=k_tanh[n][:], in_=tanh_y[n][:], func=ACT.Copy, scale=ck[:, CHUNKS + j : CHUNKS + j + 1]
+                )
+
+        def kt_vector(n):
+            g, j = units[n]
+            nc.vector.tensor_scalar(
+                out=k_tanh[n][:], in0=tanh_y[n][:], scalar1=ck[:, CHUNKS + j : CHUNKS + j + 1], scalar2=None, op0=ALU.mult
             )
 
         def make_h(n):
@@ -382,6 +390,8 @@ def tile_extendedinfomaxicarelativegrad_w4_kernel(
             if n == last:
                 at(n, READ_Y, make_f, n - 1, 1)
             if pe_sum(n):
+                if n in KT_DVE:
+                    at(n - 1, STORE, kt_vector, n)
                 at(n, TURN, turn_sum, n)
                 at(n + 1, READ_SUM, group_f, n)
             else:
@@ -409,7 +419,7 @@ def tile_extendedinfomaxicarelativegrad_w4_kernel(
         for i, tag, step in ((0, "side1", 11), (1, "side2", 11), (2, "side0", ROW2)):
             piece = (i, 1, 0, EARLY_CHUNKS)
             at(step, MX, multiply, piece, tag, 1, [0, 1])
-            at(early - 1, MX, multiply, piece, tag, 1, [2])
+            at(max(step, early - 1), MX, multiply, piece, tag, 1, [2])
         for i in (1, 0, 2):
             piece = (i, 1, 0, EARLY_CHUNKS)
             at(G3, MX, multiply, piece, None, 1, [3])

@@ -21,23 +21,17 @@ ALU = mybir.AluOpType
 ACT = mybir.ActivationFunctionType
 
 P = 128
-PASS = 512
+PACK = 4
+PASS = P * PACK
 GROUPS = N // PASS
 D_PASSES = D // PASS
 CHUNKS = M // P
+BANK_BLOCKS = PASS // P
+
 EARLY_CHUNKS = 4
-PE_SUM_UNITS = 12
-PLAIN_SLOTS = (0,)
-SPLIT0 = 1
-KT_DVE = range(8, 12)
-A1_STEP = -7
-A0_STEP = -6
-E3 = 1
-QF_EARLY = 99
-R6 = 1
-R7 = 0
-G3 = 18
-ROW2 = 13
+SUMMED_UNITS = 12
+K_TANH_ON_VECTOR = range(8, 10)
+PLAIN_TURN_UNTIL = 8
 
 
 def tile_extendedinfomaxicarelativegrad_w4_kernel(
@@ -49,18 +43,21 @@ def tile_extendedinfomaxicarelativegrad_w4_kernel(
     with ExitStack() as ctx:
         keep = ctx.enter_context(tc.tile_pool(name="keep", bufs=1))
         work = ctx.enter_context(tc.tile_pool(name="work", bufs=3))
-        psum = ctx.enter_context(tc.psum_pool(name="psum", bufs=3))
+        psum = ctx.enter_context(tc.psum_pool(name="psum", bufs=1))
         ctx.enter_context(tc.manual_schedule())
+
+        def bank(tag, shape, dtype=F32):
+            return psum.tile(shape, dtype, name="bank_" + tag, tag=tag, bufs=3 if tag == "y_bank" else 1)
 
         ident = keep.tile([P, P], F32)
         ident_bf = keep.tile([P, P], BF16)
         root_ident = keep.tile([P, P], F32)
         ck_rows = keep.tile([P, P], BF16)
         ck = keep.tile([P, 2 * CHUNKS], F32)
-        scale_cols = keep.tile([P, 8], F32)
+        scale_cols = keep.tile([P, D_PASSES * PACK], F32)
         scale_spread = keep.tile([P, D], F32)
-        a_cols = keep.tile([P, GROUPS * 4], BF16)
-        b_cols = keep.tile([P, GROUPS * 4], BF16)
+        a_cols = keep.tile([P, GROUPS * PACK], BF16)
+        b_cols = keep.tile([P, GROUPS * PACK], BF16)
         a_spread = keep.tile([P, N], BF16)
         b_spread = keep.tile([P, N], BF16)
         w_codes = keep.tile([P, D_PASSES, 2 * M], U8, align_bytes=64)
@@ -74,94 +71,92 @@ def tile_extendedinfomaxicarelativegrad_w4_kernel(
 
         x_raw = {}
 
-        def load_x(g, u):
-            x_raw[g, u] = keep.tile([P, 2, D], U8, name="x_raw_%d_%d" % (g, u))
-            rows = x_bytes[g * PASS : (g + 1) * PASS, :].rearrange("(p t) d -> p t d", t=4)
-            nc.sync.dma_start(out=x_raw[g, u][:], in_=rows[:, 2 * u : 2 * u + 2, :])
+        def load_x(g):
+            rows = x_bytes[g * PASS : (g + 1) * PASS, :].rearrange("(p t) d -> p t d", t=PACK)
+            for u in range(2):
+                x_raw[g, u] = keep.tile([P, 2, D], U8, name="x_raw_%d_%d" % (g, u))
+                nc.sync.dma_start(out=x_raw[g, u][:], in_=rows[:, 2 * u : 2 * u + 2, :])
 
         nc.vector.memset(ck_rows[:], 0.0)
-        nc.vector.memset(w_plane[:].rearrange("p g n -> p (g n)").bitcast(I32), 0)
+        nc.vector.memset(w_plane[:].rearrange("p s n -> p (s n)").bitcast(I32), 0)
         make_identity(nc, ident[:])
         make_identity(nc, ident_bf[:])
+        nc.gpsimd.tensor_scalar(
+            out=root_ident[:], in0=ident[:], scalar1=root_n, scalar2=0.0, op0=ALU.mult, op1=ALU.add
+        )
 
         nc.sync.dma_start(
-            out=scale_cols[:].rearrange("p (s t) -> p s t", t=4),
-            in_=x_scale.rearrange("o (s p t) -> p (o s) t", p=P, t=4),
+            out=scale_cols[:].rearrange("p (s t) -> p s t", t=PACK),
+            in_=x_scale.rearrange("o (s p t) -> p (o s) t", p=P, t=PACK),
         )
-        load_x(0, 0)
-        load_x(0, 1)
-        nc.sync.dma_start(
-            out=b_cols[:].rearrange("p (g t) -> p g t", t=4), in_=b.rearrange("(g p t) -> p g t", p=P, t=4)
-        )
-        nc.sync.dma_start(
-            out=a_cols[:].rearrange("p (g t) -> p g t", t=4), in_=a.rearrange("(g p t) -> p g t", p=P, t=4)
-        )
+        load_x(0)
+        for cols, vector in ((b_cols, b), (a_cols, a)):
+            nc.sync.dma_start(
+                out=cols[:].rearrange("p (g t) -> p g t", t=PACK), in_=vector.rearrange("(g p t) -> p g t", p=P, t=PACK)
+            )
         nc.sync.dma_start(out=ck_rows[0:CHUNKS, :], in_=c.rearrange("(j p) -> j p", p=P))
         nc.sync.dma_start(out=ck_rows[CHUNKS : 2 * CHUNKS, :], in_=k.rearrange("(j p) -> j p", p=P))
-        nc.sync.dma_start(out=w_codes[:].bitcast(I32), in_=w_words.rearrange("g p n -> p g n").bitcast(I32))
-        load_x(1, 0)
-        load_x(1, 1)
+        nc.sync.dma_start(out=w_codes[:].bitcast(I32), in_=w_words.rearrange("s p n -> p s n").bitcast(I32))
+        load_x(1)
         for q in range(4):
             nc.sync.dma_start(
                 out=w_plane[32 * q : 32 * q + 4, :, :].bitcast(I32),
-                in_=w_scales[:, 4 * q : 4 * q + 4, :].rearrange("g r n -> r g n").bitcast(I32),
+                in_=w_scales[:, 4 * q : 4 * q + 4, :].rearrange("s r n -> r s n").bitcast(I32),
             )
         for g in range(2, GROUPS):
-            load_x(g, 0)
-            load_x(g, 1)
+            load_x(g)
 
-        def spread_bank(cols, first, tag):
-            bank = psum.tile([P, 4, P], F32, tag=tag, bufs=1)
-            for i in range(4):
-                nc.tensor.transpose(bank[:, i, :], cols[:, first + i : first + i + 1].to_broadcast([P, P]), ident[:])
-            return bank
+        def spread(cols, first, tag):
+            spread_bank = bank(tag, [P, PACK, P])
+            for i in range(PACK):
+                column = cols[:, first + i : first + i + 1].to_broadcast([P, P])
+                nc.tensor.transpose(spread_bank[:, i, :], column, ident[:])
+            return spread_bank
 
-        for half in range(2):
-            bank = spread_bank(scale_cols, 4 * half, "turn%d" % half)
-            dst = scale_spread[:, PASS * half : PASS * (half + 1)].rearrange("q (p j) -> q p j", j=4)
-            if half == 1:
-                nc.scalar.activation(out=dst, in_=bank[:].rearrange("q j p -> q p j"), func=ACT.Copy)
-            else:
-                nc.vector.tensor_copy(out=dst, in_=bank[:].rearrange("q j p -> q p j"))
+        for s, copy_out in enumerate((nc.vector.tensor_copy, partial(nc.scalar.activation, func=ACT.Copy))):
+            copy_out(
+                out=scale_spread[:, PASS * s : PASS * (s + 1)].rearrange("q (p t) -> q p t", t=PACK),
+                in_=spread(scale_cols, PACK * s, "turn%d" % s)[:].rearrange("q t p -> q p t"),
+            )
 
-        def spread_pairs(cols, spread, half, tag):
-            bank = spread_bank(cols[:].bitcast(F32), 4 * half, tag)
+        def spread_tokens(cols, target, half, tag):
+            words = spread(cols[:].bitcast(F32), PACK * half, tag)
             nc.scalar.copy(
-                out=spread[:].bitcast(F32)[:, PASS * half : PASS * (half + 1)], in_=bank[:].rearrange("q i p -> q (i p)")
+                out=target[:].bitcast(F32)[:, PASS * half : PASS * (half + 1)], in_=words[:].rearrange("q i p -> q (i p)")
             )
 
         def turn_ck():
-            bank = psum.tile([P, P], BF16, tag="turn1", bufs=1)
-            nc.tensor.transpose(bank[:], ck_rows[:], ident_bf[:])
-            nc.scalar.copy(out=ck[:], in_=bank[:, 0 : 2 * CHUNKS])
+            ck_bank = bank("turn1", [P, P], BF16)
+            nc.tensor.transpose(ck_bank[:], ck_rows[:], ident_bf[:])
+            nc.scalar.copy(out=ck[:], in_=ck_bank[:, 0 : 2 * CHUNKS])
 
         x_wide, x_grouped, x_bank = {}, {}, {}
 
-        def scale_x(g, t):
+        def scale_x(g, t, cols):
             u, e = divmod(t, 2)
-            if e == 0:
+            if (g, u) not in x_wide:
                 x_wide[g, u] = work.tile([P, 2, D], BF16, name="x_wide")
-            for cols in (slice(0, PASS), slice(PASS, D)) if (g, t) == (0, 0) and SPLIT0 else (slice(0, D),):
-                nc.vector.tensor_tensor(
-                    out=x_wide[g, u][:, e, cols], in0=x_raw[g, u][:, e, cols].bitcast(FP8),
-                    in1=scale_spread[:, cols], op=ALU.mult,
-                )
+            nc.vector.tensor_tensor(
+                out=x_wide[g, u][:, e, cols], in0=x_raw[g, u][:, e, cols].bitcast(FP8), in1=scale_spread[:, cols],
+                op=ALU.mult,
+            )
 
         def turn_x(g, u, s):
             words = x_wide[g, u][:].bitcast(F32)
-            x_bank[g, u, s] = psum.tile([P, 4, P], F32, name="x_bank", tag="side%d" % (1 + s), bufs=1)
+            half = PASS // 2
+            x_bank[g, u, s] = bank("side%d" % (1 + s), [P, PACK, P])
             for e in range(2):
                 for v in range(2):
                     nc.tensor.transpose(
-                        x_bank[g, u, s][:, 2 * e + v, :], words[:, e, 256 * s + v : 256 * (s + 1) : 2], ident[:]
+                        x_bank[g, u, s][:, 2 * e + v, :], words[:, e, half * s + v : half * (s + 1) : 2], ident[:]
                     )
 
         def group_x(g, u, s):
             if u == 0:
-                x_grouped[g, s] = work.tile([P, 4 * PASS], BF16, name="x_grouped", bufs=4, align_bytes=64)
-            dst = x_grouped[g, s][:].bitcast(F32)[:, PASS * u : PASS * (u + 1)]
+                x_grouped[g, s] = work.tile([P, PACK * PASS], BF16, name="x_grouped", bufs=4, align_bytes=64)
+            words = x_grouped[g, s][:].bitcast(F32)[:, PASS * u : PASS * (u + 1)]
             nc.scalar.copy(
-                out=dst.rearrange("p (q j) -> p q j", j=4), in_=x_bank[g, u, s][:].rearrange("p j q -> p q j")
+                out=words.rearrange("p (q i) -> p q i", i=PACK), in_=x_bank[g, u, s][:].rearrange("p i q -> p q i")
             )
 
         def quantize_x(g, s):
@@ -172,24 +167,32 @@ def tile_extendedinfomaxicarelativegrad_w4_kernel(
 
         units = [(g, j) for g in range(GROUPS) for j in range(EARLY_CHUNKS)]
         units = units + [(g, j) for j in range(EARLY_CHUNKS, CHUNKS) for g in range(GROUPS)]
-        y_bank, tanh_y, y_full, k_tanh, summed = {}, {}, {}, {}, {}
-        pair_tiles, turned = {}, {}
+        y_psum, tanh_y, y_full, k_tanh, summed, turned, pair_tiles = {}, {}, {}, {}, {}, {}, {}
 
-        def pe_sum(n):
-            return n < PE_SUM_UNITS
-
-        def pair_tile(name, n, dtype, count=1):
+        def halves(name, n, dtype, count=1):
             key = (name, n // 2)
             if key not in pair_tiles:
                 pair_tiles[key] = work.tile([P, 2 * PASS], dtype, name=name, align_bytes=64)
             return pair_tiles[key][:, PASS * (n % 2) : PASS * (n % 2 + count)]
 
-        def project(n):
+        def c_col(n):
+            j = units[n][1]
+            return ck[:, j : j + 1]
+
+        def k_col(n):
+            j = CHUNKS + units[n][1]
+            return ck[:, j : j + 1]
+
+        def tokens(target, n, count=1):
+            g = units[n][0]
+            return target[:, g * PASS : (g + count) * PASS]
+
+        def project(n, tag):
             g, j = units[n]
-            y_bank[n] = psum.tile([P, PASS], F32, name="y_bank")
+            y_psum[n] = bank(tag, [P, PASS])
             for s in range(D_PASSES):
                 nc.tensor.matmul_mx(
-                    out=y_bank[n][:],
+                    out=y_psum[n][:],
                     lhsT=w_codes[:, s, 2 * P * j : 2 * P * (j + 1)].bitcast(FP4X4),
                     lhsT_scale=w_plane[:, s, P * j : P * (j + 1)],
                     rhs=x_codes[:, s, g * PASS : (g + 1) * PASS].bitcast(FP8X4),
@@ -198,82 +201,93 @@ def tile_extendedinfomaxicarelativegrad_w4_kernel(
                     stop=(s == D_PASSES - 1),
                 )
 
-        def activate(n):
-            g, j = units[n]
-            c_col = ck[:, j : j + 1]
-            tanh_y[n] = work.tile([P, PASS], F32, name="tanh_y")
-            if not pe_sum(n):
-                nc.scalar.activation(out=tanh_y[n][:], in_=y_bank[n][:], func=ACT.Tanh, bias=c_col)
-                return
-            by_slot = y_bank[n][:].rearrange("m (u p e) -> m u e p", u=2, e=2)
-            y_full[n] = work.tile([P, PASS], F32, name="y_full")
-            k_tanh[n] = work.tile([P, PASS], F32, name="k_tanh")
-            nc.scalar.activation(
-                out=tanh_y[n][:].rearrange("m (u e p) -> m u e p", u=2, e=2), in_=by_slot, func=ACT.Tanh, bias=c_col
-            )
-            nc.scalar.activation(
-                out=y_full[n][:].rearrange("m (u e p) -> m u e p", u=2, e=2), in_=by_slot, func=ACT.Identity, bias=c_col
-            )
-            if n not in KT_DVE:
-                nc.scalar.activation(
-                    out=k_tanh[n][:], in_=tanh_y[n][:], func=ACT.Copy, scale=ck[:, CHUNKS + j : CHUNKS + j + 1]
-                )
-
-        def kt_vector(n):
-            g, j = units[n]
-            nc.vector.tensor_scalar(
-                out=k_tanh[n][:], in0=tanh_y[n][:], scalar1=ck[:, CHUNKS + j : CHUNKS + j + 1], scalar2=None, op0=ALU.mult
-            )
-
         def make_h(n):
-            g, j = units[n]
             nc.vector.scalar_tensor_tensor(
-                out=pair_tile("h_rows", n, BF16), in0=y_bank[n][:], scalar=ck[:, j : j + 1],
-                in1=b_spread[:, g * PASS : (g + 1) * PASS], op0=ALU.add, op1=ALU.mult,
+                out=halves("h_rows", n, BF16), in0=y_psum[n][:], scalar=c_col(n), in1=tokens(b_spread, n),
+                op0=ALU.add, op1=ALU.mult,
             )
+
+        def make_tanh(n):
+            tanh_y[n] = work.tile([P, PASS], F32, name="tanh_y")
+            nc.scalar.activation(out=tanh_y[n][:], in_=y_psum[n][:], func=ACT.Tanh, bias=c_col(n))
 
         def make_u(n):
-            g, j = units[n]
             nc.vector.scalar_tensor_tensor(
-                out=pair_tile("u_sum", n, F32), in0=tanh_y[n][:], scalar=ck[:, CHUNKS + j : CHUNKS + j + 1],
-                in1=y_bank[n][:], op0=ALU.mult, op1=ALU.add,
+                out=halves("u_sum", n, F32), in0=tanh_y[n][:], scalar=k_col(n), in1=y_psum[n][:],
+                op0=ALU.mult, op1=ALU.add,
             )
 
         def make_f(n, count):
-            g, j = units[n]
             nc.vector.scalar_tensor_tensor(
-                out=pair_tile("f_rows", n, BF16, count), in0=pair_tile("u_sum", n, F32, count), scalar=ck[:, j : j + 1],
-                in1=a_spread[:, g * PASS : (g + count) * PASS], op0=ALU.add, op1=ALU.mult,
+                out=halves("f_rows", n, BF16, count), in0=halves("u_sum", n, F32, count), scalar=c_col(n),
+                in1=tokens(a_spread, n, count), op0=ALU.add, op1=ALU.mult,
+            )
+
+        def make_terms(n):
+            by_slot = y_psum[n][:].rearrange("m (u p e) -> m u e p", u=2, e=2)
+            tanh_y[n] = work.tile([P, PASS], F32, name="tanh_y")
+            y_full[n] = work.tile([P, PASS], F32, name="y_full")
+            for term, func in ((tanh_y[n], ACT.Tanh), (y_full[n], ACT.Identity)):
+                nc.scalar.activation(
+                    out=term[:].rearrange("m (u e p) -> m u e p", u=2, e=2), in_=by_slot, func=func, bias=c_col(n)
+                )
+
+        def make_k_tanh(n):
+            k_tanh[n] = work.tile([P, PASS], F32, name="k_tanh")
+            if n in K_TANH_ON_VECTOR:
+                nc.vector.tensor_scalar(out=k_tanh[n][:], in0=tanh_y[n][:], scalar1=k_col(n), scalar2=None, op0=ALU.mult)
+            else:
+                nc.scalar.activation(out=k_tanh[n][:], in_=tanh_y[n][:], func=ACT.Copy, scale=k_col(n))
+
+        def turn_sum(n):
+            summed[n] = bank("turn%d" % (n % 2), [P, PACK, P])
+            for t in range(PACK):
+                for term, opens in ((y_full[n], True), (k_tanh[n], False)):
+                    plain = opens and t == 0 and n < PLAIN_TURN_UNTIL
+                    nc.tensor.matmul(
+                        out=summed[n][:, t, :], lhsT=term[:, P * t : P * (t + 1)], rhs=ident[:],
+                        is_transpose=not plain, start=opens, stop=not opens,
+                    )
+
+        def group_sum(n):
+            g = units[n][0]
+            nc.vector.tensor_tensor(
+                out=halves("f_grouped", n, BF16).rearrange("p (m t) -> p m t", t=PACK),
+                in0=summed[n][:].rearrange("p t m -> p m t"),
+                in1=a_cols[:, PACK * g : PACK * (g + 1)].unsqueeze(1).to_broadcast([P, P, PACK]),
+                op=ALU.mult,
+            )
+
+        def keep_y(n):
+            for name, func in (("tanh_kept", ACT.Tanh), ("y_kept", ACT.Identity)):
+                nc.scalar.activation(out=halves(name, n, F32), in_=y_psum[n][:], func=func, bias=c_col(n))
+
+        def kept_h(n):
+            nc.vector.tensor_tensor(
+                out=halves("h_rows", n, BF16, 2), in0=halves("y_kept", n, F32, 2), in1=tokens(b_spread, n, 2), op=ALU.mult
+            )
+
+        def kept_u(n):
+            nc.vector.scalar_tensor_tensor(
+                out=halves("u_sum", n, F32, 2), in0=halves("tanh_kept", n, F32, 2), scalar=k_col(n),
+                in1=halves("y_kept", n, F32, 2), op0=ALU.mult, op1=ALU.add,
+            )
+
+        def kept_f(n):
+            nc.vector.tensor_tensor(
+                out=halves("f_rows", n, BF16, 2), in0=halves("u_sum", n, F32, 2), in1=tokens(a_spread, n, 2), op=ALU.mult
             )
 
         def turn_pair(which, n, tag):
-            words = pair_tile(which + "_rows", n, BF16, 2).bitcast(F32)
-            turned[which, n] = psum.tile([P, 4, P], F32, name="turned", tag=tag, bufs=1)
-            for i in range(4):
+            words = halves(which + "_rows", n, BF16, 2).bitcast(F32)
+            turned[which, n] = bank(tag, [P, PACK, P])
+            for i in range(PACK):
                 nc.tensor.transpose(turned[which, n][:, i, :], words[:, P * i : P * (i + 1)], ident[:])
 
         def group_pair(which, n):
             nc.scalar.copy(
-                out=pair_tile(which + "_grouped", n, BF16, 2).bitcast(F32).rearrange("p (i m u) -> p i m u", i=2, u=2),
+                out=halves(which + "_grouped", n, BF16, 2).bitcast(F32).rearrange("p (i m u) -> p i m u", i=2, u=2),
                 in_=turned[which, n][:].rearrange("p (i u) m -> p i m u", u=2),
-            )
-
-        def turn_sum(n):
-            summed[n] = psum.tile([P, 4, P], F32, name="summed", tag="turn%d" % (n % 2), bufs=1)
-            for t in range(4):
-                for term, first in ((y_full[n], True), (k_tanh[n], False)):
-                    nc.tensor.matmul(
-                        out=summed[n][:, t, :], lhsT=term[:, P * t : P * (t + 1)], rhs=ident[:],
-                        is_transpose=not (first and t in PLAIN_SLOTS), start=first, stop=not first,
-                    )
-
-        def group_f(n):
-            g, j = units[n]
-            nc.vector.tensor_tensor(
-                out=pair_tile("f_grouped", n, BF16).rearrange("p (m t) -> p m t", t=4),
-                in0=summed[n][:].rearrange("p t m -> p m t"),
-                in1=a_cols[:, 4 * g : 4 * g + 4].unsqueeze(1).to_broadcast([P, P, 4]),
-                op=ALU.mult,
             )
 
         def quantize_f(n, count):
@@ -281,7 +295,7 @@ def tile_extendedinfomaxicarelativegrad_w4_kernel(
             cols = slice(P * g, P * (g + count))
             nc.vector.quantize_mx(
                 out=f_codes[:, j, cols].bitcast(FP8X4), scales=f_plane[:, j, cols],
-                in_=pair_tile("f_grouped", n, BF16, count),
+                in_=halves("f_grouped", n, BF16, count),
             )
 
         def quantize_h(n, count):
@@ -289,184 +303,202 @@ def tile_extendedinfomaxicarelativegrad_w4_kernel(
             cols = slice(P * j, P * (j + count))
             nc.vector.quantize_mx(
                 out=h_codes[:, g, cols].bitcast(FP8X4), scales=h_plane[:, g, cols],
-                in_=pair_tile("h_grouped", n, BF16, count),
+                in_=halves("h_grouped", n, BF16, count),
             )
 
-        out_bank, result = {}, {}
+        out_psum, result = {}, {}
 
-        def mx_pass(dst, i, j0, count, g):
-            rows, cols = slice(P * g, P * (g + 1)), slice(P * j0, P * (j0 + count))
-            nc.tensor.matmul_mx(
-                out=dst,
-                lhsT=f_codes[:, i, rows].bitcast(FP8X4),
-                lhsT_scale=f_plane[:, i, rows],
-                rhs=h_codes[:, g, cols].bitcast(FP8X4),
-                rhs_scale=h_plane[:, g, cols],
-                start=(g == 0),
-                stop=(g == GROUPS - 1),
-            )
-
-        def multiply(piece, tag, bufs, groups, blocks=None):
+        def multiply(piece, tag, groups):
             i0, rows, j0, cols = piece
-            if piece not in out_bank:
-                out_bank[piece] = psum.tile([P, PASS], F32, name="out_bank", tag=tag, bufs=bufs)
-            for i in blocks or range(rows):
+            if piece not in out_psum:
+                out_psum[piece] = bank(tag, [P, PASS])
+            h_cols = slice(P * j0, P * (j0 + cols))
+            for i in range(rows):
                 for g in groups:
-                    mx_pass(out_bank[piece][:, P * i : P * (i + cols)], i0 + i, j0, cols, g)
-
-        def diagonal(piece):
-            i0, rows, j0, cols = piece
-            hits = [i + j for i in range(rows) for j in range(cols) if i0 + i == j0 + j]
-            return hits[0] if hits else None
-
-        def scale_out(piece, first, last, on_vector=False):
-            if last > first:
-                cols = slice(P * first, P * last)
-                if on_vector:
-                    nc.vector.tensor_scalar(
-                        out=result[piece][:, cols], in0=out_bank[piece][:, cols], scalar1=-1.0 / root_n, scalar2=None,
-                        op0=ALU.mult,
-                    )
-                else:
-                    nc.scalar.activation(
-                        out=result[piece][:, cols], in_=out_bank[piece][:, cols], func=ACT.Copy, scale=-1.0 / root_n
+                    f_cols = slice(P * g, P * (g + 1))
+                    nc.tensor.matmul_mx(
+                        out=out_psum[piece][:, P * i : P * (i + cols)],
+                        lhsT=f_codes[:, i0 + i, f_cols].bitcast(FP8X4),
+                        lhsT_scale=f_plane[:, i0 + i, f_cols],
+                        rhs=h_codes[:, g, h_cols].bitcast(FP8X4),
+                        rhs_scale=h_plane[:, g, h_cols],
+                        start=(g == 0),
+                        stop=(g == GROUPS - 1),
                     )
 
-        def empty(piece, on_vector=False):
-            count = piece[1] * piece[3]
+        def new_result(piece):
             result[piece] = work.tile([P, PASS], F32, name="result", bufs=8)
-            d = diagonal(piece)
-            if d is None or not on_vector:
-                scale_out(piece, 0, count, on_vector)
-            else:
-                scale_out(piece, 0, d, on_vector)
-                scale_out(piece, d + 1, count, on_vector)
 
-        def store(piece, on_vector):
+        def empty(piece):
+            width = P * piece[1] * piece[3]
+            new_result(piece)
+            nc.scalar.activation(
+                out=result[piece][:, 0:width], in_=out_psum[piece][:, 0:width], func=ACT.Copy, scale=-1.0 / root_n
+            )
+
+        def store(piece):
             i0, rows, j0, cols = piece
-            d = diagonal(piece)
-            if d is not None and not on_vector:
-                block = result[piece][:, P * d : P * (d + 1)]
+            nc.sync.dma_start(
+                out=out[P * i0 : P * (i0 + rows), P * j0 : P * (j0 + cols)].rearrange("(i p) n -> p i n", p=P),
+                in_=result[piece][:, 0 : P * rows * cols].rearrange("p (i n) -> p i n", i=rows),
+            )
+
+        def add_identity_and_store(piece):
+            i0, rows, j0, cols = piece
+            for place in [i + j for i in range(rows) for j in range(cols) if i0 + i == j0 + j]:
+                block = result[piece][:, P * place : P * (place + 1)]
                 nc.gpsimd.tensor_tensor(out=block, in0=block, in1=root_ident[:], op=ALU.add)
-            elif d is not None:
-                nc.vector.scalar_tensor_tensor(
-                    out=result[piece][:, P * d : P * (d + 1)], in0=out_bank[piece][:, P * d : P * (d + 1)],
-                    scalar=-1.0 / root_n, in1=root_ident[:], op0=ALU.mult, op1=ALU.add,
-                )
-            dst = out[P * i0 : P * (i0 + rows), P * j0 : P * (j0 + cols)].rearrange("(i p) n -> p i n", p=P)
-            nc.sync.dma_start(out=dst, in_=result[piece][:, 0 : P * rows * cols].rearrange("p (i n) -> p i n", i=rows))
+            store(piece)
 
-        nc.gpsimd.tensor_scalar(
-            out=root_ident[:], in0=ident[:], scalar1=root_n, scalar2=0.0, op0=ALU.mult, op1=ALU.add
-        )
+        def finish_corner(piece):
+            plain = slice(0, PASS - P)
+            corner = slice(PASS - P, PASS)
+            new_result(piece)
+            nc.vector.tensor_scalar(
+                out=result[piece][:, plain], in0=out_psum[piece][:, plain], scalar1=-1.0 / root_n, scalar2=None,
+                op0=ALU.mult,
+            )
+            nc.vector.scalar_tensor_tensor(
+                out=result[piece][:, corner], in0=out_psum[piece][:, corner], scalar=-1.0 / root_n, in1=root_ident[:],
+                op0=ALU.mult, op1=ALU.add,
+            )
+            store(piece)
 
-        TURN, PROJECT, MX, TANH, GROUP, EMPTY, READ_Y, READ_SUM, SCALE_X, QUANT_H, MAKE_F, QUANT, STORE = range(13)
+        TURN, PROJECT, MULTIPLY, TANH, GROUP, EMPTY, READ_Y, READ_SUM, SCALE_X, QUANT_H, MAKE_F, QUANT, LAST = range(13)
         plan = defaultdict(list)
 
-        def at(step, slot, fn, *args):
-            plan[step, slot].append(partial(fn, *args))
+        def at(step, stage, fn, *args):
+            plan[step, stage].append(partial(fn, *args))
+
+        def turn_and_group(step, which, n, tag):
+            at(step, TURN, turn_pair, which, n, tag)
+            at(step, GROUP, group_pair, which, n)
+
+        def finish(step, piece, stage=EMPTY):
+            at(step, stage, empty, piece)
+            at(step, LAST, add_identity_and_store, piece)
 
         for g in range(GROUPS):
-            first = EARLY_CHUNKS * g
-            for t in range(4):
-                at(first - 9 + t, SCALE_X, scale_x, g, t)
+            first_projection = EARLY_CHUNKS * g - 2
+            for t in range(PACK):
+                widths = [slice(0, PASS), slice(PASS, D)] if (g, t) == (0, 0) else [slice(0, D)]
+                for cols in widths:
+                    at(first_projection - 7 + t, SCALE_X, scale_x, g, t, cols)
             for u in range(2):
                 for s in range(D_PASSES):
-                    at(first - 7 + 2 * u + s, TURN, turn_x, g, u, s)
-                    at(first - 7 + 2 * u + s, GROUP, group_x, g, u, s)
+                    at(first_projection - 5 + 2 * u + s, TURN, turn_x, g, u, s)
+                    at(first_projection - 5 + 2 * u + s, GROUP, group_x, g, u, s)
             for s in range(D_PASSES):
-                at(first - 4 + s, QUANT, quantize_x, g, s)
-        at(-9, GROUP, spread_pairs, b_cols, b_spread, 0, "side0")
-        at(-9, GROUP, spread_pairs, b_cols, b_spread, 1, "turn0")
-        at(-8, GROUP, turn_ck)
-        at(A1_STEP, GROUP, spread_pairs, a_cols, a_spread, 1, "side0")
-        at(A0_STEP, GROUP, spread_pairs, a_cols, a_spread, 0, "turn0")
+                at(first_projection - 2 + s, QUANT, quantize_x, g, s)
+        start = min(step for step, stage in plan)
+        at(start, GROUP, spread_tokens, b_cols, b_spread, 0, "side0")
+        at(start, GROUP, spread_tokens, b_cols, b_spread, 1, "turn0")
+        at(start + 1, GROUP, turn_ck)
+        at(start + 2, GROUP, spread_tokens, a_cols, a_spread, 1, "side0")
+        at(start + 3, GROUP, spread_tokens, a_cols, a_spread, 0, "turn0")
 
-        last = len(units) - 1
-        for n in range(len(units)):
-            at(n - 2, PROJECT, project, n)
-            at(n - 1, TANH, activate, n)
+        kept = len(units) - GROUPS
+        for n in range(kept):
+            at(n - 2, PROJECT, project, n, "y_bank")
             at(n, READ_Y, make_h, n)
-            if n == last:
-                at(n, READ_Y, make_f, n - 1, 1)
-            if pe_sum(n):
-                if n in KT_DVE:
-                    at(n - 1, STORE, kt_vector, n)
+            if n < SUMMED_UNITS:
+                at(n - 1, TANH, make_terms, n)
+                at(n - 1, LAST if n in K_TANH_ON_VECTOR else TANH, make_k_tanh, n)
                 at(n, TURN, turn_sum, n)
-                at(n + 1, READ_SUM, group_f, n)
+                at(n + 1, READ_SUM, group_sum, n)
             else:
+                at(n - 1, TANH, make_tanh, n)
                 at(n, READ_Y, make_u, n)
-        for n in range(0, len(units), 2):
-            same_chunk = units[n][1] == units[n + 1][1]
-            whole, halves = [(n, 2)], [(n, 1), (n + 1, 1)]
-            at(n + 2, TURN, turn_pair, "h", n, "side0" if pe_sum(n) else "turn1")
-            at(n + 2, GROUP, group_pair, "h", n)
-            if not pe_sum(n):
-                for part in halves[1:] if n + 1 == last else whole if same_chunk else halves:
+        for n in range(0, kept, 2):
+            whole, apart = [(n, 2)], [(n, 1), (n + 1, 1)]
+            f_parts, h_parts = (whole, apart) if units[n][1] == units[n + 1][1] else (apart, whole)
+            if n < SUMMED_UNITS:
+                turn_and_group(n + 2, "h", n, "side0")
+            else:
+                turn_and_group(n + 2, "h", n, "turn1")
+                for part in f_parts:
                     at(n + 1, MAKE_F, make_f, *part)
-                at(n + 2, TURN, turn_pair, "f", n, "turn0")
-                at(n + 2, GROUP, group_pair, "f", n)
-            for part in halves if same_chunk else whole:
-                at(n + 3, QUANT_H, quantize_h, *part)
-            for part in whole if same_chunk else halves:
-                at(n + 3, QUANT_H if n >= QF_EARLY else QUANT, quantize_f, *part)
+                turn_and_group(n + 2, "f", n, "turn0")
+            hurry = n + 2 == kept
+            for part in h_parts:
+                at(n + 3 - hurry, QUANT_H, quantize_h, *part)
+            for part in f_parts:
+                at(n + 3 - hurry, QUANT_H if hurry else QUANT, quantize_f, *part)
 
-        def finish(step, piece, on_vector=False):
-            at(step, STORE if on_vector else EMPTY, empty, piece, on_vector)
-            at(step, STORE, store, piece, on_vector)
+        for i in range(GROUPS):
+            step = SUMMED_UNITS + max(0, 2 * i - 1)
+            at(step, PROJECT, project, kept + i, "side0" if i else "side1")
+            at(step, EMPTY, keep_y, kept + i)
 
         early = EARLY_CHUNKS * GROUPS
-        for i, tag, step in ((0, "side1", 11), (1, "side2", 11), (2, "side0", ROW2)):
-            piece = (i, 1, 0, EARLY_CHUNKS)
-            at(step, MX, multiply, piece, tag, 1, [0, 1])
-            at(max(step, early - 1), MX, multiply, piece, tag, 1, [2])
-        for i in (1, 0, 2):
-            piece = (i, 1, 0, EARLY_CHUNKS)
-            at(G3, MX, multiply, piece, None, 1, [3])
-            finish(G3 + 1, piece)
-        piece = (3, 1, 0, EARLY_CHUNKS)
-        at(early + 5, MX, multiply, piece, "side2", 1, range(GROUPS))
-        finish(early + 6, piece)
-        for j in range(EARLY_CHUNKS, CHUNKS - 1):
-            first = GROUPS * j
-            row_pieces, done = [], 0
-            for width in (4, 2, 1):
-                if j + 1 - done >= width and len(row_pieces) < 2:
-                    row_pieces.append((j, 1, done, width))
-                    done = done + width
-            hurry = j == CHUNKS - 2
-            col_rows = j if done == j + 1 else j + 1
-            full, rest = (0, 4, j, 1), (4, col_rows - 4, j, 1)
-            if not hurry:
-                at(first + 7, MX, multiply, full, "side2", 1, range(GROUPS))
-                finish(first + 8 + E3 % 2, full)
-                if rest[1]:
-                    at(first + 9 + min(E3, 1), MX, multiply, rest, "side2", 1, range(GROUPS))
-                    finish(first + 10 + min(E3, 1), rest)
-            for r, piece in enumerate(row_pieces):
-                at(first + 5, MX, multiply, piece, "side%d" % r, 1, [0, 1])
-                at(first + 7 - hurry, MX, multiply, piece, "side%d" % r, 1, [2, 3])
-                finish(first + 8 - hurry, piece)
-            if hurry:
-                at(first + 6, MX, multiply, full, "y_bank", 3, range(GROUPS))
-                at(first + 7 + R6, MX, multiply, rest, "side2", 1, range(GROUPS))
-                finish(first + 7, full)
-                finish(first + 8 + R6, rest)
-        j = CHUNKS - 1
-        row_pieces = [(j, 1, 0, 4), (j, 1, 4, 4)]
-        col_pieces = [(0, 4, j, 1), (4, 3, j, 1)]
-        end = len(units) + 2
-        for r, piece in enumerate(row_pieces):
-            at(end - 2 + R7, MX, multiply, piece, "side%d" % r, 1, [0, 1])
-        at(end, MX, multiply, col_pieces[0], "y_bank", 3, range(GROUPS))
-        for piece in reversed(row_pieces):
-            at(end, MX, multiply, piece, None, None, [2, 3])
-        at(end, MX, multiply, col_pieces[1], "y_bank", 3, range(GROUPS))
-        finish(end + 1, col_pieces[0])
-        finish(end + 1, row_pieces[1], True)
-        finish(end + 1, row_pieces[0])
-        finish(end + 2, col_pieces[1], True)
+        square = [(i, 1, 0, EARLY_CHUNKS) for i in range(EARLY_CHUNKS)]
+        at(early - 1, MULTIPLY, multiply, square[0], "side1", range(GROUPS - 1))
+        at(early - 1, MULTIPLY, multiply, square[1], "side2", range(GROUPS - 1))
+        at(early + 2, MULTIPLY, multiply, square[2], "side0", range(GROUPS - 1))
+        for i, tag in ((1, "side2"), (0, "side1"), (2, "side0")):
+            at(early + 2, MULTIPLY, multiply, square[i], tag, [GROUPS - 1])
+            finish(early + 3, square[i])
+        at(early + 5, MULTIPLY, multiply, square[3], "side2", range(GROUPS))
+        finish(early + 6, square[3])
 
-        for step, slot in sorted(plan):
-            for fn in plan[step, slot]:
-                fn()
+        def pieces_of(j):
+            width = max(w for w in (4, 2, 1) if w <= j + 1 - BANK_BLOCKS)
+            row = [(j, 1, 0, BANK_BLOCKS), (j, 1, BANK_BLOCKS, width)]
+            height = j if BANK_BLOCKS + width == j + 1 else j + 1
+            column = [(i0, min(BANK_BLOCKS, height - i0), j, 1) for i0 in range(0, height, BANK_BLOCKS)]
+            return row, column
+
+        def multiply_row(row, first_step, second_step):
+            for r, piece in enumerate(row):
+                at(first_step, MULTIPLY, multiply, piece, "side%d" % r, [0, 1])
+                at(second_step, MULTIPLY, multiply, piece, "side%d" % r, [2, 3])
+                finish(second_step + 1, piece)
+
+        n = GROUPS * EARLY_CHUNKS
+        row, column = pieces_of(EARLY_CHUNKS)
+        at(n + 7, MULTIPLY, multiply, column[0], "side2", range(GROUPS))
+        finish(n + 9, column[0])
+        multiply_row(row, n + 5, n + 7)
+        n = n + GROUPS
+        row, column = pieces_of(EARLY_CHUNKS + 1)
+        multiply_row(row, n + 5, n + 6)
+        at(n + 7, MULTIPLY, multiply, column[0], "side2", range(GROUPS))
+        finish(n + 7, column[0], LAST)
+        at(n + 8, MULTIPLY, multiply, column[1], "side2", range(GROUPS))
+        finish(n + 9, column[1])
+        n = n + GROUPS
+        row, column = pieces_of(CHUNKS - 2)
+        multiply_row(row, n + 4, n + 5)
+        for r, piece in enumerate(column):
+            at(n + 6, MULTIPLY, multiply, piece, "y_bank", range(GROUPS))
+            finish(n + 7, piece)
+
+        n = kept
+        row, column = pieces_of(CHUNKS - 1)
+        for i in range(2):
+            at(n + i, READ_Y, kept_h, n + 2 * i)
+            turn_and_group(n + 1 + i, "h", n + 2 * i, "turn%d" % (1 - i))
+            for half in range(2):
+                at(n + 1 + i, QUANT, quantize_h, n + 2 * i + half, 1)
+        at(n + 1, MAKE_F, kept_u, n)
+        at(n + 2, MAKE_F, kept_f, n)
+        turn_and_group(n + 3, "f", n, "turn1")
+        at(n + 3, MULTIPLY, multiply, column[0], "y_bank", range(GROUPS))
+        at(n + 3, READ_Y, kept_u, n + 2)
+        at(n + 3, QUANT_H, quantize_f, n, 2)
+        at(n + 3, MAKE_F, kept_f, n + 2)
+        for r, piece in enumerate(row):
+            at(n + 4, MULTIPLY, multiply, piece, "side%d" % r, [0, 1])
+        finish(n + 4, column[0])
+        turn_and_group(n + 5, "f", n + 2, "turn0")
+        at(n + 5, MULTIPLY, multiply, column[1], "side2", range(GROUPS))
+        at(n + 5, QUANT, quantize_f, n + 2, 2)
+        for r in (1, 0):
+            at(n + 6, MULTIPLY, multiply, row[r], "side%d" % r, [2, 3])
+        finish(n + 6, column[1])
+        at(n + 7, LAST, finish_corner, row[1])
+        finish(n + 7, row[0])
+
+        for key in sorted(plan):
+            for call in plan[key]:
+                call()

import math
from collections import defaultdict
from contextlib import ExitStack
from functools import partial

import concourse.mybir as mybir
from concourse.masks import make_identity

N, D, M = 2048, 1024, 1024
FLOPS = 2 * N * D * M + 2 * N * M * M

F32 = mybir.dt.float32
BF16 = mybir.dt.bfloat16
I32 = mybir.dt.int32
U32 = mybir.dt.uint32
U8 = mybir.dt.uint8
FP8 = mybir.dt.float8_e4m3fn
FP8X4 = mybir.dt.float8_e4m3fn_x4
FP4X4 = mybir.dt.float4_e2m1fn_x4
ALU = mybir.AluOpType
ACT = mybir.ActivationFunctionType

P = 128
PACK = 4
PASS = P * PACK
GROUPS = N // PASS
D_PASSES = D // PASS
CHUNKS = M // P
BANK_BLOCKS = PASS // P

EARLY_CHUNKS = 4
SUMMED_UNITS = 12
K_TANH_ON_VECTOR = range(8, 10)
PLAIN_TURN_UNTIL = 8


def tile_extendedinfomaxicarelativegrad_w4_kernel(
    tc, x_bytes, x_scale, w_words, w_scales, c, k, a, b, out
):
    nc = tc.nc
    root_n = math.sqrt(N)

    with ExitStack() as ctx:
        keep = ctx.enter_context(tc.tile_pool(name="keep", bufs=1))
        work = ctx.enter_context(tc.tile_pool(name="work", bufs=3))
        psum = ctx.enter_context(tc.psum_pool(name="psum", bufs=1))
        ctx.enter_context(tc.manual_schedule())

        def bank(tag, shape, dtype=F32):
            return psum.tile(shape, dtype, name="bank_" + tag, tag=tag, bufs=3 if tag == "y_bank" else 1)

        ident = keep.tile([P, P], F32)
        ident_bf = keep.tile([P, P], BF16)
        root_ident = keep.tile([P, P], F32)
        ck_rows = keep.tile([P, P], BF16)
        ck = keep.tile([P, 2 * CHUNKS], F32)
        scale_cols = keep.tile([P, D_PASSES * PACK], F32)
        scale_spread = keep.tile([P, D], F32)
        a_cols = keep.tile([P, GROUPS * PACK], BF16)
        b_cols = keep.tile([P, GROUPS * PACK], BF16)
        a_spread = keep.tile([P, N], BF16)
        b_spread = keep.tile([P, N], BF16)
        w_codes = keep.tile([P, D_PASSES, 2 * M], U8, align_bytes=64)
        w_plane = keep.tile([P, D_PASSES, M], U8, align_bytes=64)
        x_codes = keep.tile([P, D_PASSES, N], U32, align_bytes=64)
        x_plane = keep.tile([P, D_PASSES, N], U8, align_bytes=64)
        f_codes = keep.tile([P, CHUNKS, GROUPS * P], U32, align_bytes=64)
        f_plane = keep.tile([P, CHUNKS, GROUPS * P], U8, align_bytes=64)
        h_codes = keep.tile([P, GROUPS, M], U32, align_bytes=64)
        h_plane = keep.tile([P, GROUPS, M], U8, align_bytes=64)

        x_raw = {}

        def load_x(g):
            rows = x_bytes[g * PASS : (g + 1) * PASS, :].rearrange("(p t) d -> p t d", t=PACK)
            for u in range(2):
                x_raw[g, u] = keep.tile([P, 2, D], U8, name="x_raw_%d_%d" % (g, u))
                nc.sync.dma_start(out=x_raw[g, u][:], in_=rows[:, 2 * u : 2 * u + 2, :])

        nc.vector.memset(ck_rows[:], 0.0)
        nc.vector.memset(w_plane[:].rearrange("p s n -> p (s n)").bitcast(I32), 0)
        make_identity(nc, ident[:])
        make_identity(nc, ident_bf[:])
        nc.gpsimd.tensor_scalar(
            out=root_ident[:], in0=ident[:], scalar1=root_n, scalar2=0.0, op0=ALU.mult, op1=ALU.add
        )

        nc.sync.dma_start(
            out=scale_cols[:].rearrange("p (s t) -> p s t", t=PACK),
            in_=x_scale.rearrange("o (s p t) -> p (o s) t", p=P, t=PACK),
        )
        load_x(0)
        for cols, vector in ((b_cols, b), (a_cols, a)):
            nc.sync.dma_start(
                out=cols[:].rearrange("p (g t) -> p g t", t=PACK), in_=vector.rearrange("(g p t) -> p g t", p=P, t=PACK)
            )
        nc.sync.dma_start(out=ck_rows[0:CHUNKS, :], in_=c.rearrange("(j p) -> j p", p=P))
        nc.sync.dma_start(out=ck_rows[CHUNKS : 2 * CHUNKS, :], in_=k.rearrange("(j p) -> j p", p=P))
        nc.sync.dma_start(out=w_codes[:].bitcast(I32), in_=w_words.rearrange("s p n -> p s n").bitcast(I32))
        load_x(1)
        for q in range(4):
            nc.sync.dma_start(
                out=w_plane[32 * q : 32 * q + 4, :, :].bitcast(I32),
                in_=w_scales[:, 4 * q : 4 * q + 4, :].rearrange("s r n -> r s n").bitcast(I32),
            )
        for g in range(2, GROUPS):
            load_x(g)

        def spread(cols, first, tag):
            spread_bank = bank(tag, [P, PACK, P])
            for i in range(PACK):
                column = cols[:, first + i : first + i + 1].to_broadcast([P, P])
                nc.tensor.transpose(spread_bank[:, i, :], column, ident[:])
            return spread_bank

        for s, copy_out in enumerate((nc.vector.tensor_copy, partial(nc.scalar.activation, func=ACT.Copy))):
            copy_out(
                out=scale_spread[:, PASS * s : PASS * (s + 1)].rearrange("q (p t) -> q p t", t=PACK),
                in_=spread(scale_cols, PACK * s, "turn%d" % s)[:].rearrange("q t p -> q p t"),
            )

        def spread_tokens(cols, target, half, tag):
            words = spread(cols[:].bitcast(F32), PACK * half, tag)
            nc.scalar.copy(
                out=target[:].bitcast(F32)[:, PASS * half : PASS * (half + 1)], in_=words[:].rearrange("q i p -> q (i p)")
            )

        def turn_ck():
            ck_bank = bank("turn1", [P, P], BF16)
            nc.tensor.transpose(ck_bank[:], ck_rows[:], ident_bf[:])
            nc.scalar.copy(out=ck[:], in_=ck_bank[:, 0 : 2 * CHUNKS])

        x_wide, x_grouped, x_bank = {}, {}, {}

        def scale_x(g, t, cols):
            u, e = divmod(t, 2)
            if (g, u) not in x_wide:
                x_wide[g, u] = work.tile([P, 2, D], BF16, name="x_wide")
            nc.vector.tensor_tensor(
                out=x_wide[g, u][:, e, cols], in0=x_raw[g, u][:, e, cols].bitcast(FP8), in1=scale_spread[:, cols],
                op=ALU.mult,
            )

        def turn_x(g, u, s):
            words = x_wide[g, u][:].bitcast(F32)
            half = PASS // 2
            x_bank[g, u, s] = bank("side%d" % (1 + s), [P, PACK, P])
            for e in range(2):
                for v in range(2):
                    nc.tensor.transpose(
                        x_bank[g, u, s][:, 2 * e + v, :], words[:, e, half * s + v : half * (s + 1) : 2], ident[:]
                    )

        def group_x(g, u, s):
            if u == 0:
                x_grouped[g, s] = work.tile([P, PACK * PASS], BF16, name="x_grouped", bufs=4, align_bytes=64)
            words = x_grouped[g, s][:].bitcast(F32)[:, PASS * u : PASS * (u + 1)]
            nc.scalar.copy(
                out=words.rearrange("p (q i) -> p q i", i=PACK), in_=x_bank[g, u, s][:].rearrange("p i q -> p q i")
            )

        def quantize_x(g, s):
            cols = slice(g * PASS, (g + 1) * PASS)
            nc.vector.quantize_mx(
                out=x_codes[:, s, cols].bitcast(FP8X4), scales=x_plane[:, s, cols], in_=x_grouped[g, s][:]
            )

        units = [(g, j) for g in range(GROUPS) for j in range(EARLY_CHUNKS)]
        units = units + [(g, j) for j in range(EARLY_CHUNKS, CHUNKS) for g in range(GROUPS)]
        y_psum, tanh_y, y_full, k_tanh, summed, turned, pair_tiles = {}, {}, {}, {}, {}, {}, {}

        def halves(name, n, dtype, count=1):
            key = (name, n // 2)
            if key not in pair_tiles:
                pair_tiles[key] = work.tile([P, 2 * PASS], dtype, name=name, align_bytes=64)
            return pair_tiles[key][:, PASS * (n % 2) : PASS * (n % 2 + count)]

        def c_col(n):
            j = units[n][1]
            return ck[:, j : j + 1]

        def k_col(n):
            j = CHUNKS + units[n][1]
            return ck[:, j : j + 1]

        def tokens(target, n, count=1):
            g = units[n][0]
            return target[:, g * PASS : (g + count) * PASS]

        def project(n, tag):
            g, j = units[n]
            y_psum[n] = bank(tag, [P, PASS])
            for s in range(D_PASSES):
                nc.tensor.matmul_mx(
                    out=y_psum[n][:],
                    lhsT=w_codes[:, s, 2 * P * j : 2 * P * (j + 1)].bitcast(FP4X4),
                    lhsT_scale=w_plane[:, s, P * j : P * (j + 1)],
                    rhs=x_codes[:, s, g * PASS : (g + 1) * PASS].bitcast(FP8X4),
                    rhs_scale=x_plane[:, s, g * PASS : (g + 1) * PASS],
                    start=(s == 0),
                    stop=(s == D_PASSES - 1),
                )

        def make_h(n):
            nc.vector.scalar_tensor_tensor(
                out=halves("h_rows", n, BF16), in0=y_psum[n][:], scalar=c_col(n), in1=tokens(b_spread, n),
                op0=ALU.add, op1=ALU.mult,
            )

        def make_tanh(n):
            tanh_y[n] = work.tile([P, PASS], F32, name="tanh_y")
            nc.scalar.activation(out=tanh_y[n][:], in_=y_psum[n][:], func=ACT.Tanh, bias=c_col(n))

        def make_u(n):
            nc.vector.scalar_tensor_tensor(
                out=halves("u_sum", n, F32), in0=tanh_y[n][:], scalar=k_col(n), in1=y_psum[n][:],
                op0=ALU.mult, op1=ALU.add,
            )

        def make_f(n, count):
            nc.vector.scalar_tensor_tensor(
                out=halves("f_rows", n, BF16, count), in0=halves("u_sum", n, F32, count), scalar=c_col(n),
                in1=tokens(a_spread, n, count), op0=ALU.add, op1=ALU.mult,
            )

        def make_terms(n):
            by_slot = y_psum[n][:].rearrange("m (u p e) -> m u e p", u=2, e=2)
            tanh_y[n] = work.tile([P, PASS], F32, name="tanh_y")
            y_full[n] = work.tile([P, PASS], F32, name="y_full")
            for term, func in ((tanh_y[n], ACT.Tanh), (y_full[n], ACT.Identity)):
                nc.scalar.activation(
                    out=term[:].rearrange("m (u e p) -> m u e p", u=2, e=2), in_=by_slot, func=func, bias=c_col(n)
                )

        def make_k_tanh(n):
            k_tanh[n] = work.tile([P, PASS], F32, name="k_tanh")
            if n in K_TANH_ON_VECTOR:
                nc.vector.tensor_scalar(out=k_tanh[n][:], in0=tanh_y[n][:], scalar1=k_col(n), scalar2=None, op0=ALU.mult)
            else:
                nc.scalar.activation(out=k_tanh[n][:], in_=tanh_y[n][:], func=ACT.Copy, scale=k_col(n))

        def turn_sum(n):
            summed[n] = bank("turn%d" % (n % 2), [P, PACK, P])
            for t in range(PACK):
                for term, opens in ((y_full[n], True), (k_tanh[n], False)):
                    plain = opens and t == 0 and n < PLAIN_TURN_UNTIL
                    nc.tensor.matmul(
                        out=summed[n][:, t, :], lhsT=term[:, P * t : P * (t + 1)], rhs=ident[:],
                        is_transpose=not plain, start=opens, stop=not opens,
                    )

        def group_sum(n):
            g = units[n][0]
            nc.vector.tensor_tensor(
                out=halves("f_grouped", n, BF16).rearrange("p (m t) -> p m t", t=PACK),
                in0=summed[n][:].rearrange("p t m -> p m t"),
                in1=a_cols[:, PACK * g : PACK * (g + 1)].unsqueeze(1).to_broadcast([P, P, PACK]),
                op=ALU.mult,
            )

        def keep_y(n):
            for name, func in (("tanh_kept", ACT.Tanh), ("y_kept", ACT.Identity)):
                nc.scalar.activation(out=halves(name, n, F32), in_=y_psum[n][:], func=func, bias=c_col(n))

        def kept_h(n):
            nc.vector.tensor_tensor(
                out=halves("h_rows", n, BF16, 2), in0=halves("y_kept", n, F32, 2), in1=tokens(b_spread, n, 2), op=ALU.mult
            )

        def kept_u(n):
            nc.vector.scalar_tensor_tensor(
                out=halves("u_sum", n, F32, 2), in0=halves("tanh_kept", n, F32, 2), scalar=k_col(n),
                in1=halves("y_kept", n, F32, 2), op0=ALU.mult, op1=ALU.add,
            )

        def kept_f(n):
            nc.vector.tensor_tensor(
                out=halves("f_rows", n, BF16, 2), in0=halves("u_sum", n, F32, 2), in1=tokens(a_spread, n, 2), op=ALU.mult
            )

        def turn_pair(which, n, tag):
            words = halves(which + "_rows", n, BF16, 2).bitcast(F32)
            turned[which, n] = bank(tag, [P, PACK, P])
            for i in range(PACK):
                nc.tensor.transpose(turned[which, n][:, i, :], words[:, P * i : P * (i + 1)], ident[:])

        def group_pair(which, n):
            nc.scalar.copy(
                out=halves(which + "_grouped", n, BF16, 2).bitcast(F32).rearrange("p (i m u) -> p i m u", i=2, u=2),
                in_=turned[which, n][:].rearrange("p (i u) m -> p i m u", u=2),
            )

        def quantize_f(n, count):
            g, j = units[n]
            cols = slice(P * g, P * (g + count))
            nc.vector.quantize_mx(
                out=f_codes[:, j, cols].bitcast(FP8X4), scales=f_plane[:, j, cols],
                in_=halves("f_grouped", n, BF16, count),
            )

        def quantize_h(n, count):
            g, j = units[n]
            cols = slice(P * j, P * (j + count))
            nc.vector.quantize_mx(
                out=h_codes[:, g, cols].bitcast(FP8X4), scales=h_plane[:, g, cols],
                in_=halves("h_grouped", n, BF16, count),
            )

        out_psum, result = {}, {}

        def multiply(piece, tag, groups):
            i0, rows, j0, cols = piece
            if piece not in out_psum:
                out_psum[piece] = bank(tag, [P, PASS])
            h_cols = slice(P * j0, P * (j0 + cols))
            for i in range(rows):
                for g in groups:
                    f_cols = slice(P * g, P * (g + 1))
                    nc.tensor.matmul_mx(
                        out=out_psum[piece][:, P * i : P * (i + cols)],
                        lhsT=f_codes[:, i0 + i, f_cols].bitcast(FP8X4),
                        lhsT_scale=f_plane[:, i0 + i, f_cols],
                        rhs=h_codes[:, g, h_cols].bitcast(FP8X4),
                        rhs_scale=h_plane[:, g, h_cols],
                        start=(g == 0),
                        stop=(g == GROUPS - 1),
                    )

        def new_result(piece):
            result[piece] = work.tile([P, PASS], F32, name="result", bufs=8)

        def empty(piece):
            width = P * piece[1] * piece[3]
            new_result(piece)
            nc.scalar.activation(
                out=result[piece][:, 0:width], in_=out_psum[piece][:, 0:width], func=ACT.Copy, scale=-1.0 / root_n
            )

        def store(piece):
            i0, rows, j0, cols = piece
            nc.sync.dma_start(
                out=out[P * i0 : P * (i0 + rows), P * j0 : P * (j0 + cols)].rearrange("(i p) n -> p i n", p=P),
                in_=result[piece][:, 0 : P * rows * cols].rearrange("p (i n) -> p i n", i=rows),
            )

        def add_identity_and_store(piece):
            i0, rows, j0, cols = piece
            for place in [i + j for i in range(rows) for j in range(cols) if i0 + i == j0 + j]:
                block = result[piece][:, P * place : P * (place + 1)]
                nc.gpsimd.tensor_tensor(out=block, in0=block, in1=root_ident[:], op=ALU.add)
            store(piece)

        def finish_corner(piece):
            plain = slice(0, PASS - P)
            corner = slice(PASS - P, PASS)
            new_result(piece)
            nc.vector.tensor_scalar(
                out=result[piece][:, plain], in0=out_psum[piece][:, plain], scalar1=-1.0 / root_n, scalar2=None,
                op0=ALU.mult,
            )
            nc.vector.scalar_tensor_tensor(
                out=result[piece][:, corner], in0=out_psum[piece][:, corner], scalar=-1.0 / root_n, in1=root_ident[:],
                op0=ALU.mult, op1=ALU.add,
            )
            store(piece)

        TURN, PROJECT, MULTIPLY, TANH, GROUP, EMPTY, READ_Y, READ_SUM, SCALE_X, QUANT_H, MAKE_F, QUANT, LAST = range(13)
        plan = defaultdict(list)

        def at(step, stage, fn, *args):
            plan[step, stage].append(partial(fn, *args))

        def turn_and_group(step, which, n, tag):
            at(step, TURN, turn_pair, which, n, tag)
            at(step, GROUP, group_pair, which, n)

        def finish(step, piece, stage=EMPTY):
            at(step, stage, empty, piece)
            at(step, LAST, add_identity_and_store, piece)

        for g in range(GROUPS):
            first_projection = EARLY_CHUNKS * g - 2
            for t in range(PACK):
                widths = [slice(0, PASS), slice(PASS, D)] if (g, t) == (0, 0) else [slice(0, D)]
                for cols in widths:
                    at(first_projection - 7 + t, SCALE_X, scale_x, g, t, cols)
            for u in range(2):
                for s in range(D_PASSES):
                    at(first_projection - 5 + 2 * u + s, TURN, turn_x, g, u, s)
                    at(first_projection - 5 + 2 * u + s, GROUP, group_x, g, u, s)
            for s in range(D_PASSES):
                at(first_projection - 2 + s, QUANT, quantize_x, g, s)
        start = min(step for step, stage in plan)
        at(start, GROUP, spread_tokens, b_cols, b_spread, 0, "side0")
        at(start, GROUP, spread_tokens, b_cols, b_spread, 1, "turn0")
        at(start + 1, GROUP, turn_ck)
        at(start + 2, GROUP, spread_tokens, a_cols, a_spread, 1, "side0")
        at(start + 3, GROUP, spread_tokens, a_cols, a_spread, 0, "turn0")

        kept = len(units) - GROUPS
        for n in range(kept):
            at(n - 2, PROJECT, project, n, "y_bank")
            at(n, READ_Y, make_h, n)
            if n < SUMMED_UNITS:
                at(n - 1, TANH, make_terms, n)
                at(n - 1, LAST if n in K_TANH_ON_VECTOR else TANH, make_k_tanh, n)
                at(n, TURN, turn_sum, n)
                at(n + 1, READ_SUM, group_sum, n)
            else:
                at(n - 1, TANH, make_tanh, n)
                at(n, READ_Y, make_u, n)
        for n in range(0, kept, 2):
            whole, apart = [(n, 2)], [(n, 1), (n + 1, 1)]
            f_parts, h_parts = (whole, apart) if units[n][1] == units[n + 1][1] else (apart, whole)
            if n < SUMMED_UNITS:
                turn_and_group(n + 2, "h", n, "side0")
            else:
                turn_and_group(n + 2, "h", n, "turn1")
                for part in f_parts:
                    at(n + 1, MAKE_F, make_f, *part)
                turn_and_group(n + 2, "f", n, "turn0")
            hurry = n + 2 == kept
            for part in h_parts:
                at(n + 3 - hurry, QUANT_H, quantize_h, *part)
            for part in f_parts:
                at(n + 3 - hurry, QUANT_H if hurry else QUANT, quantize_f, *part)

        for i in range(GROUPS):
            step = SUMMED_UNITS + max(0, 2 * i - 1)
            at(step, PROJECT, project, kept + i, "side0" if i else "side1")
            at(step, EMPTY, keep_y, kept + i)

        early = EARLY_CHUNKS * GROUPS
        square = [(i, 1, 0, EARLY_CHUNKS) for i in range(EARLY_CHUNKS)]
        at(early - 1, MULTIPLY, multiply, square[0], "side1", range(GROUPS - 1))
        at(early - 1, MULTIPLY, multiply, square[1], "side2", range(GROUPS - 1))
        at(early + 2, MULTIPLY, multiply, square[2], "side0", range(GROUPS - 1))
        for i, tag in ((1, "side2"), (0, "side1"), (2, "side0")):
            at(early + 2, MULTIPLY, multiply, square[i], tag, [GROUPS - 1])
            finish(early + 3, square[i])
        at(early + 5, MULTIPLY, multiply, square[3], "side2", range(GROUPS))
        finish(early + 6, square[3])

        def pieces_of(j):
            width = max(w for w in (4, 2, 1) if w <= j + 1 - BANK_BLOCKS)
            row = [(j, 1, 0, BANK_BLOCKS), (j, 1, BANK_BLOCKS, width)]
            height = j if BANK_BLOCKS + width == j + 1 else j + 1
            column = [(i0, min(BANK_BLOCKS, height - i0), j, 1) for i0 in range(0, height, BANK_BLOCKS)]
            return row, column

        def multiply_row(row, first_step, second_step):
            for r, piece in enumerate(row):
                at(first_step, MULTIPLY, multiply, piece, "side%d" % r, [0, 1])
                at(second_step, MULTIPLY, multiply, piece, "side%d" % r, [2, 3])
                finish(second_step + 1, piece)

        n = GROUPS * EARLY_CHUNKS
        row, column = pieces_of(EARLY_CHUNKS)
        at(n + 7, MULTIPLY, multiply, column[0], "side2", range(GROUPS))
        finish(n + 9, column[0])
        multiply_row(row, n + 5, n + 7)
        n = n + GROUPS
        row, column = pieces_of(EARLY_CHUNKS + 1)
        multiply_row(row, n + 5, n + 6)
        at(n + 7, MULTIPLY, multiply, column[0], "side2", range(GROUPS))
        finish(n + 7, column[0], LAST)
        at(n + 8, MULTIPLY, multiply, column[1], "side2", range(GROUPS))
        finish(n + 9, column[1])
        n = n + GROUPS
        row, column = pieces_of(CHUNKS - 2)
        multiply_row(row, n + 4, n + 5)
        for r, piece in enumerate(column):
            at(n + 6, MULTIPLY, multiply, piece, "y_bank", range(GROUPS))
            finish(n + 7, piece)

        n = kept
        row, column = pieces_of(CHUNKS - 1)
        for i in range(2):
            at(n + i, READ_Y, kept_h, n + 2 * i)
            turn_and_group(n + 1 + i, "h", n + 2 * i, "turn%d" % (1 - i))
            for half in range(2):
                at(n + 1 + i, QUANT, quantize_h, n + 2 * i + half, 1)
        at(n + 1, MAKE_F, kept_u, n)
        at(n + 2, MAKE_F, kept_f, n)
        turn_and_group(n + 3, "f", n, "turn1")
        at(n + 3, MULTIPLY, multiply, column[0], "y_bank", range(GROUPS))
        at(n + 3, READ_Y, kept_u, n + 2)
        at(n + 3, QUANT_H, quantize_f, n, 2)
        at(n + 3, MAKE_F, kept_f, n + 2)
        for r, piece in enumerate(row):
            at(n + 4, MULTIPLY, multiply, piece, "side%d" % r, [0, 1])
        finish(n + 4, column[0])
        turn_and_group(n + 5, "f", n + 2, "turn0")
        at(n + 5, MULTIPLY, multiply, column[1], "side2", range(GROUPS))
        at(n + 5, QUANT, quantize_f, n + 2, 2)
        for r in (1, 0):
            at(n + 6, MULTIPLY, multiply, row[r], "side%d" % r, [2, 3])
        finish(n + 6, column[1])
        at(n + 7, LAST, finish_corner, row[1])
        finish(n + 7, row[0])

        for key in sorted(plan):
            for call in plan[key]:
                call()
